import numpy as np
import ml_dtypes


def mxq(x, axis, fmt="e4m3"):
    dtype, down = {"e4m3": (ml_dtypes.float8_e4m3fn, 7), "e5m2": (ml_dtypes.float8_e5m2, 14)}[fmt]
    v = np.moveaxis(np.asarray(x, np.float32).astype(ml_dtypes.bfloat16).astype(np.float64), axis, -1)
    blocks = v.reshape(v.shape[:-1] + (-1, 32))
    amax = np.abs(blocks).max(-1, keepdims=True)
    byte = np.maximum(np.where(amax > 0, np.frexp(amax)[1] - 1 + 127, 0) - down, 1)
    scale = np.exp2(byte - 127.0)
    codes = (blocks / scale).astype(np.float32).astype(dtype).astype(np.float64)
    return np.moveaxis((codes * scale).reshape(v.shape), -1, axis)


WIDE = False


def mx_kscale(k):
    if not WIDE:
        return np.ones(k)
    levels = np.array([10, -10, 5, -5, 0])
    if k % 512:
        return np.exp2(np.random.permutation(np.resize(levels, k // 32))).repeat(32)
    a = np.empty((k // 512, 16))
    for p in range(k // 512):
        a[p, :8] = np.random.permutation(np.resize(levels, 8))
        for g in range(8):
            far = levels[np.abs(levels - a[p, g]) >= 10]
            a[p, g + 8] = far[np.random.randint(len(far))]
    return np.exp2(a.ravel()).repeat(32)


BF16 = ml_dtypes.bfloat16


def bf(x):
    return np.asarray(x, np.float32).astype(BF16)


def f64(x):
    return np.asarray(x).astype(np.float64)


E2M1 = np.array([0.0, 0.5, 1.0, 1.5, 2.0, 3.0, 4.0, 6.0, -0.0, -0.5, -1.0, -1.5, -2.0, -3.0, -4.0, -6.0])


def pack_weight(w, fmt):
    k, n = w.shape
    w = f64(bf(w)).reshape(k // 32, 32, n)
    amax = np.abs(w).max(1)
    if fmt == "e4m3":
        byte = np.frexp(amax)[1] - 1 + 127 - 7
    else:
        mant, ex = np.frexp(amax / 6.0)
        byte = np.where(mant > 0.5, ex, ex - 1) + 127
    byte = np.clip(np.where(amax > 0, byte, 1), 1, 254)
    scaled = (w * np.exp2(127.0 - byte)[:, None, :]).reshape(k, n).astype(np.float32)
    by_word = np.ascontiguousarray(scaled.reshape(k // 512, 128, 4, n).transpose(0, 1, 3, 2))
    if fmt == "e4m3":
        words = by_word.astype(ml_dtypes.float8_e4m3fn).view(np.uint8)
    else:
        c = by_word.astype(ml_dtypes.float4_e2m1fn).view(np.uint8) & 0xF
        words = c[..., 0::2] | (c[..., 1::2] << 4)
    return np.ascontiguousarray(words), np.ascontiguousarray(byte.astype(np.uint8).reshape(k // 512, 16, n))


def unpack_weight(words, scales, fmt):
    g, p, n, _ = words.shape
    if fmt == "e4m3":
        vals = np.ascontiguousarray(words).view(ml_dtypes.float8_e4m3fn).astype(np.float64)
    else:
        nib = np.empty((g, p, n, 4), np.uint8)
        nib[..., 0::2] = words & 0xF
        nib[..., 1::2] = words >> 4
        vals = E2M1[nib]
    vals = vals * np.repeat(np.exp2(scales.astype(np.float64) - 127.0), 8, axis=1)[..., None]
    return vals.transpose(0, 1, 3, 2).reshape(g * 512, n)
def pack4(w):
    words, scales = pack_weight(w, "e2m1")
    return words.reshape(words.shape[0], 128, -1), scales


def unpack4(words, scales):
    return unpack_weight(words.reshape(words.shape[0], 128, -1, 2), scales, "e2m1")


def planes(Y):
    n, m = Y.shape
    b = f64(bf(Y)).reshape(n // 32, 32, m)
    amax = np.abs(b).max(1)
    byte = np.clip(np.where(amax > 0, np.frexp(amax)[1] - 1 + 127 - 7, 1), 1, 254)
    codes = (b * np.exp2(127.0 - byte)[:, None, :]).reshape(n, m).astype(np.float32).astype(ml_dtypes.float8_e4m3fn).view(np.uint8)
    words = codes.reshape(n // 512, 128, 4, m).transpose(0, 1, 3, 2)
    return np.ascontiguousarray(words), np.ascontiguousarray(byte.astype(np.uint8).reshape(n // 512, 16, m))


N, D, F = 1024, 1024, 1024

EPS_RESIDUAL = 0.3


def setup_inputs():
    s = mx_kscale(D)
    t = mx_kscale(N)
    x = bf(np.random.standard_normal((N, D)) * s[None, :])
    w_words, w_scales = pack4(np.random.standard_normal((D, F)) / np.sqrt(D) / s[:, None])
    return {
        "x": x,
        "w_words": w_words,
        "w_scales": w_scales,
        "adj": bf(np.random.standard_normal((N, N)) / np.sqrt(N) * t[None, :]),
        "a1": bf(np.random.standard_normal(F) / np.sqrt(F)),
        "a2": bf(np.random.standard_normal(F) / np.sqrt(F)),
        "ri": bf((1.0 + 0.1 * np.random.standard_normal(N)) / t),
        "ro": bf(1.0 + 0.1 * np.random.standard_normal(N)),
    }


def signed_gate(z, a1, a2):
    s = np.sum(z * a1[None, :], axis=-1)
    t = np.sum(z * a2[None, :], axis=-1)
    return np.tanh(s[:, None] + t[None, :])


def core(x, w_words, w_scales, adj, a1, a2, ri, ro):
    z = mxq(f64(x), 1, "e4m3") @ unpack4(w_words, w_scales)
    c = f64(adj) * signed_gate(z, f64(a1), f64(a2))
    zs = z * f64(ri)[:, None]
    m = mxq(c, 1, "e4m3") @ mxq(zs, 0, "e4m3")
    return EPS_RESIDUAL * z + f64(ro)[:, None] * m


def reference(x, w_words, w_scales, adj, a1, a2, ri, ro):
    R_out = core(x, w_words, w_scales, adj, a1, a2, ri, ro)
    words, scales = planes(R_out)
    return R_out, words, scales

@@ -1,0 +1,523 @@
+from contextlib import ExitStack
+
+import concourse.mybir as mybir
+from concourse.masks import make_identity
+
+F32 = mybir.dt.float32
+BF16 = mybir.dt.bfloat16
+I32 = mybir.dt.int32
+U32 = mybir.dt.uint32
+U8 = mybir.dt.uint8
+FP8X4 = mybir.dt.float8_e4m3fn_x4
+FP4X4 = mybir.dt.float4_e2m1fn_x4
+MULT = mybir.AluOpType.mult
+ADD = mybir.AluOpType.add
+COPY = mybir.ActivationFunctionType.Copy
+TANH = mybir.ActivationFunctionType.Tanh
+
+FLOPS = 2 * 1024 * 1024 * 1024 * 2
+EPS = 0.3
+OFFLOAD = ()
+
+
+def tile_fagcnsignedtanhpropagation_x2_kernel(tc, x, w_words, w_scales, adj, a1, a2, ri, ro, out_0, out_1, out_2):
+    nc = tc.nc
+    with ExitStack() as ctx:
+        keep = ctx.enter_context(tc.tile_pool(name="keep", bufs=1))
+        work = ctx.enter_context(tc.tile_pool(name="work", bufs=2))
+        ps_tr = ctx.enter_context(tc.psum_pool(name="ps_tr", bufs=2))
+        ps_mm = ctx.enter_context(tc.psum_pool(name="ps_mm", bufs=4))
+        ps_s = ctx.enter_context(tc.psum_pool(name="ps_s", bufs=1))
+        ctx.enter_context(tc.manual_schedule())
+
+        x_sb = [keep.tile([128, 4, 1024], BF16, name=f"x_sb{g}", align_bytes=64) for g in range(2)]
+        adj_sb = [keep.tile([128, 4, 1024], BF16, name=f"adj_sb{g}", align_bytes=64) for g in range(2)]
+        w_codes = keep.tile([128, 2, 2048], U8, name="w_codes", align_bytes=64)
+        w_sc = keep.tile([128, 2, 1024], U8, name="w_sc", align_bytes=64)
+        a_rows = keep.tile([128, 2, 1024], BF16, name="a_rows", align_bytes=64)
+        a_bc = keep.tile([128, 2, 512], BF16, name="a_bc", align_bytes=64)
+        a_col = keep.tile([128, 4, 2], F32, name="a_col", align_bytes=64)
+        ones = keep.tile([128, 128], BF16, name="ones", align_bytes=64)
+        ident = keep.tile([128, 128], F32, name="ident", align_bytes=64)
+        ri_sb = keep.tile([128, 2, 4], BF16, name="ri_sb")
+        ro_sb = keep.tile([128, 2, 4], BF16, name="ro_sb")
+        ro32 = keep.tile([128, 2, 4], F32, name="ro32")
+        ri3 = keep.tile([128, 2, 4], F32, name="ri3")
+        dummy = keep.tile([128, 1], F32, name="dummy")
+        part = [keep.tile([128, 4, 2], F32, name=f"part{g}") for g in range(2)]
+        score = [keep.tile([128, 4, 2], F32, name=f"score{g}") for g in range(2)]
+        z03 = [keep.tile([128, 4, 1024], F32, name=f"z03_{g}", align_bytes=64) for g in range(2)]
+        xq = [keep.tile([128, 2, 128], U32, name=f"xq{s}", align_bytes=64) for s in range(8)]
+        xs = [keep.tile([128, 2, 128], U8, name=f"xs{s}", align_bytes=64) for s in range(8)]
+        zq = [keep.tile([128, 1024], U32, name=f"zq{g}", align_bytes=64) for g in range(2)]
+        zsc = [keep.tile([128, 1024], U8, name=f"zsc{g}", align_bytes=64) for g in range(2)]
+        cq = [[keep.tile([128, 512], U32, name=f"cq{j}{i}", align_bytes=64) for i in range(2)] for j in range(2)]
+        csc = [[keep.tile([128, 512], U8, name=f"csc{j}{i}", align_bytes=64) for i in range(2)] for j in range(2)]
+        o_sb = [keep.tile([128, 4, 1024], F32, name=f"o_sb{g}", align_bytes=64) for g in range(2)]
+        oq = [keep.tile([128, 1024], U32, name=f"oq{g}", align_bytes=64) for g in range(2)]
+        osc = [keep.tile([128, 1024], U8, name=f"osc{g}", align_bytes=64) for g in range(2)]
+
+        nc.vector.memset(a_rows[:], 0.0)
+        nc.gpsimd.memset(w_sc[:].bitcast(I32), 0)
+        nc.vector.memset(ones[:], 1.0)
+        nc.vector.memset(dummy[:], 0.0)
+        make_identity(nc, ident[:])
+
+        def x_view(t_dram, g):
+            return t_dram[512 * g : 512 * (g + 1), :].rearrange("(p t) k -> p t k", t=4)
+
+        def load_x(s, n=1):
+            g, t = s // 4, s % 4
+            nc.sync.dma_start(out=x_sb[g][:, t : t + n, :], in_=x_view(x, g)[:, t : t + n, :])
+
+        load_x(0)
+        for g in range(2):
+            nc.sync.dma_start(out=w_codes[:].bitcast(I32)[:, g, 0:256], in_=w_words.bitcast(I32)[g][:, 0:256])
+        load_x(1)
+        for g in range(2):
+            nc.sync.dma_start(out=w_codes[:].bitcast(I32)[:, g, 256:512], in_=w_words.bitcast(I32)[g][:, 256:512])
+        for r in range(4):
+            nc.scalar.dma_start(
+                out=w_sc[:].bitcast(I32)[r:128:32, :, :],
+                in_=w_scales.bitcast(I32).rearrange("g (q r) n -> r q g n", r=4)[r],
+            )
+        nc.scalar.dma_start(out=a_rows[0:1, 0, :], in_=a1.unsqueeze(0))
+        nc.scalar.dma_start(out=a_rows[0:1, 1, :], in_=a2.unsqueeze(0))
+        nc.scalar.activation(out=dummy[:], in_=dummy[:], func=TANH)
+        load_x(2, 2)
+        load_x(4, 2)
+        load_x(6, 2)
+        nc.sync.dma_start(out=ri_sb[:], in_=ri.rearrange("(g p t) -> p g t", g=2, t=4))
+        nc.sync.dma_start(out=ro_sb[:], in_=ro.rearrange("(g p t) -> p g t", g=2, t=4))
+        for g in range(2):
+            for h in range(2):
+                nc.sync.dma_start(out=adj_sb[g][:, 2 * h : 2 * h + 2, :], in_=x_view(adj, g)[:, 2 * h : 2 * h + 2, :])
+
+        trs = {}
+        grp = {}
+        zps = {}
+        zts = {}
+
+        def x_transpose(s):
+            g, t = s // 4, s % 4
+            words = x_sb[g][:, t, :].bitcast(F32)
+            tr = ps_tr.tile([128, 2, 2, 128], F32, name="tr")
+            for k in range(2):
+                for u in range(2):
+                    nc.tensor.transpose(tr[:, k, u, :], words[:, 256 * k + u : 256 * (k + 1) : 2], ident[:])
+            trs[s] = tr
+
+        def x_copy(s, eng):
+            xg = work.tile([128, 2, 128, 4], BF16, name="xg", align_bytes=64)
+            dst = xg[:].rearrange("p k r t -> p (k r t)").bitcast(F32).rearrange("p (k r u) -> p k r u", k=2, u=2)
+            src = trs[s][:].rearrange("p k u r -> p k r u")
+            if eng == "s":
+                nc.scalar.copy(out=dst, in_=src)
+            else:
+                nc.vector.tensor_copy(out=dst, in_=src)
+            grp[s] = xg
+
+        def x_quant(s):
+            nc.vector.quantize_mx(
+                out=xq[s][:].rearrange("p k r -> p (k r)").bitcast(FP8X4),
+                scales=xs[s][:].rearrange("p k r -> p (k r)"),
+                in_=grp[s][:].rearrange("p k r t -> p (k r t)"),
+            )
+
+        def z_mm(s, h):
+            zp = ps_mm.tile([128, 512], F32, name="mm")
+            for k in range(2):
+                nc.tensor.matmul_mx(
+                    out=zp[:],
+                    lhsT=xq[s][:, k, :].bitcast(FP8X4),
+                    lhsT_scale=xs[s][:, k, :],
+                    rhs=w_codes[:, k, 1024 * h : 1024 * (h + 1)].bitcast(FP4X4),
+                    rhs_scale=w_sc[:, k, 512 * h : 512 * (h + 1)],
+                    start=(k == 0),
+                    stop=(k == 1),
+                )
+            zps[s, h] = zp
+
+        def zt_mm(s):
+            zp = ps_mm.tile([128, 4, 128], F32, name="mm")
+            for n in range(4):
+                for k in range(2):
+                    nc.tensor.matmul_mx(
+                        out=zp[:, n, :],
+                        lhsT=w_codes[:, k, 1024 + 256 * n : 1024 + 256 * (n + 1)].bitcast(FP4X4),
+                        lhsT_scale=w_sc[:, k, 512 + 128 * n : 512 + 128 * (n + 1)],
+                        rhs=xq[s][:, k, :].bitcast(FP8X4),
+                        rhs_scale=xs[s][:, k, :],
+                        start=(k == 0),
+                        stop=(k == 1),
+                    )
+            zps[s, "t"] = zp
+
+        def zt_copy(s):
+            zt = work.tile([128, 4, 128], F32, name="zt", align_bytes=64)
+            nc.scalar.copy(out=zt[:], in_=zps[s, "t"][:])
+            zts[s] = zt
+
+        sp = [ps_s.tile([128, 512], F32, name=f"sp{g}") for g in range(2)]
+        sc = [sp[g][:, 256:264].rearrange("p (t q) -> p t q", q=2) for g in range(2)]
+
+        def zt_score(s):
+            for n in range(4):
+                nc.tensor.matmul(sc[s // 4][:, s % 4, :], lhsT=zts[s][:, n, :], rhs=a_col[:, n, :], start=(n == 0), stop=(n == 3))
+
+        def z_store(s, h):
+            g, t = s // 4, s % 4
+            nc.scalar.activation(out=z03[g][:, t, 512 * h : 512 * (h + 1)], in_=zps[s, h][:], func=COPY, scale=EPS)
+
+        def z_score(s):
+            g, t = s // 4, s % 4
+            for q in (1, 0):
+                junk = work.tile([128, 512], F32, name="junk")
+                nc.vector.scalar_tensor_tensor(
+                    out=junk[:],
+                    in0=zps[s, 0][:],
+                    scalar=1.0,
+                    in1=a_bc[:, q, :],
+                    op0=MULT,
+                    op1=MULT,
+                    accum_out=part[g][:, t, q : q + 1],
+                )
+
+        def score_sum(n):
+            g, ts = n // 2, slice(2 * (n % 2), 2 * (n % 2) + 2)
+            nc.vector.tensor_tensor(out=score[g][:, ts, :], in0=sc[g][:, ts, :], in1=part[g][:, ts, :], op=ADD)
+
+        gates = {}
+        bcast_count = [0]
+
+        def s_bcast(j, n):
+            bank = sp[bcast_count[0] % 2]
+            bcast_count[0] += 1
+            for b in range(2):
+                nc.tensor.transpose(
+                    bank[:, 128 * b : 128 * (b + 1)],
+                    score[n // 2][:, 2 * (n % 2) + b, 0:1].to_broadcast([128, 128]),
+                    ident[:],
+                )
+            gates[j, n] = bank
+
+        def gate(j, n):
+            gt = work.tile([128, 4, 256], F32, name="gate", align_bytes=64)
+            for t in range(4):
+                nc.scalar.activation(out=gt[:, t, :], in_=gates[j, n][:, 0:256], func=TANH, bias=score[j][:, t, 1:2])
+            gates[j, n] = gt
+
+        zgt = {}
+
+        def zs_piece(g, h, c, eng=nc.gpsimd):
+            if c == 0:
+                zgt[g, h] = work.tile([128, 512, 4], BF16, name="zg", align_bytes=64)
+            cols = slice(512 * h + 256 * c, 512 * h + 256 * (c + 1))
+            eng.tensor_tensor(
+                out=zgt[g, h][:, 256 * c : 256 * (c + 1), :],
+                in0=z03[g][:, :, cols].rearrange("p t f -> p f t"),
+                in1=ri3[:, g, :].unsqueeze(1).to_broadcast([128, 256, 4]),
+                op=MULT,
+            )
+
+        def zs_quant(g, h):
+            nc.vector.quantize_mx(
+                out=zq[g][:, 512 * h : 512 * (h + 1)].bitcast(FP8X4),
+                scales=zsc[g][:, 512 * h : 512 * (h + 1)],
+                in_=zgt[g, h][:].rearrange("p f t -> p (f t)"),
+            )
+
+        def adj_transpose(j, n):
+            tr = ps_tr.tile([128, 2, 256], F32, name="tr")
+            for b in range(2):
+                words = adj_sb[n // 2][:, 2 * (n % 2) + b, :].bitcast(F32)
+                for u in range(2):
+                    nc.tensor.transpose(tr[:, u, 128 * b : 128 * (b + 1)], words[:, 256 * j + u : 256 * (j + 1) : 2], ident[:])
+            trs[j, n] = tr
+
+        cgs = {}
+
+        def c_mul(j, n):
+            cg = work.tile([128, 256, 4], BF16, name="cg", align_bytes=64)
+            nc.vector.tensor_tensor(
+                out=cg[:].rearrange("p n (u e) -> p n u e", u=2),
+                in0=trs[j, n][:].rearrange("p u n -> p (u n)").bitcast(BF16).rearrange("p (u n e) -> p n u e", u=2, e=2),
+                in1=gates[j, n][:].rearrange("p (u e) n -> p n u e", u=2),
+                op=MULT,
+            )
+            cgs[j, n] = cg
+
+        def c_quant(j, n):
+            cols = slice(256 * (n % 2), 256 * (n % 2) + 256)
+            nc.vector.quantize_mx(
+                out=cq[j][n // 2][:, cols].bitcast(FP8X4),
+                scales=csc[j][n // 2][:, cols],
+                in_=cgs[j, n][:].rearrange("p n t -> p (n t)"),
+            )
+
+        mps = {}
+
+        def m_mm(g, h, t):
+            mp = ps_mm.tile([128, 512], F32, name="mm")
+            for j in range(2):
+                nc.tensor.matmul_mx(
+                    out=mp[:],
+                    lhsT=cq[j][g][:, 128 * t : 128 * (t + 1)].bitcast(FP8X4),
+                    lhsT_scale=csc[j][g][:, 128 * t : 128 * (t + 1)],
+                    rhs=zq[j][:, 512 * h : 512 * (h + 1)].bitcast(FP8X4),
+                    rhs_scale=zsc[j][:, 512 * h : 512 * (h + 1)],
+                    start=(j == 0),
+                    stop=(j == 1),
+                )
+            mps[g, h, t] = mp
+
+        def o_add(g, h, t):
+            cols = slice(512 * h, 512 * (h + 1))
+            nc.vector.scalar_tensor_tensor(
+                out=o_sb[g][:, t, cols],
+                in0=mps[g, h, t][:],
+                scalar=ro_sb[:, g, t : t + 1],
+                in1=z03[g][:, t, cols],
+                op0=MULT,
+                op1=ADD,
+            )
+
+        def o_add_split(g, h, t):
+            cols = slice(512 * h, 512 * (h + 1))
+            mr = work.tile([128, 512], F32, name="mr", align_bytes=64)
+            nc.scalar.activation(out=mr[:], in_=mps[g, h, t][:], func=COPY, scale=ro32[:, g, t : t + 1])
+            nc.gpsimd.tensor_tensor(out=o_sb[g][:, t, cols], in0=mr[:], in1=z03[g][:, t, cols], op=ADD)
+
+        def o_add_part(g, h, t, c):
+            cols = slice(512 * h + 256 * c, 512 * h + 256 * (c + 1))
+            nc.vector.scalar_tensor_tensor(
+                out=o_sb[g][:, t, cols],
+                in0=mps[g, h, t][:, 256 * c : 256 * (c + 1)],
+                scalar=ro_sb[:, g, t : t + 1],
+                in1=z03[g][:, t, cols],
+                op0=MULT,
+                op1=ADD,
+            )
+
+        ogs = {}
+
+        def o_group_part(g, h, c, n, wid, eng):
+            if (g, h) not in ogs:
+                ogs[g, h] = work.tile([128, 512, 4], BF16, name="og", align_bytes=64)
+            lo = 256 * c + wid * n
+            src = o_sb[g][:, :, 512 * h + lo : 512 * h + lo + wid].rearrange("p t f -> p f t")
+            dst = ogs[g, h][:, lo : lo + wid, :]
+            if eng == "s":
+                nc.scalar.copy(out=dst, in_=src)
+            elif eng == "g":
+                nc.gpsimd.tensor_scalar(out=dst, in0=src, scalar1=1.0, scalar2=0.0, op0=MULT, op1=ADD)
+            else:
+                nc.vector.tensor_copy(out=dst, in_=src)
+
+        def o_quant_part(g, h, c):
+            cols = slice(512 * h + 256 * c, 512 * h + 256 * (c + 1))
+            nc.vector.quantize_mx(
+                out=oq[g][:, cols].bitcast(FP8X4),
+                scales=osc[g][:, cols],
+                in_=ogs[g, h][:, 256 * c : 256 * (c + 1), :].rearrange("p n t -> p (n t)"),
+            )
+
+        def o_store_part(g, h, c):
+            cols = slice(512 * h + 256 * c, 512 * h + 256 * (c + 1))
+            nc.sync.dma_start(out=x_view(out_0, g)[:, :, cols], in_=o_sb[g][:, :, cols])
+
+        def code_store(g, lo, hi):
+            nc.sync.dma_start(
+                out=out_1[g].rearrange("p m t -> p (m t)").bitcast(I32)[:, lo:hi],
+                in_=oq[g][:, lo:hi].bitcast(I32),
+            )
+
+        def scale_store(g, lo, hi):
+            for r in range(4):
+                nc.sync.dma_start(
+                    out=out_2[g].bitcast(I32).rearrange("(q r) n -> r q n", r=4)[r][:, lo // 4 : hi // 4],
+                    in_=osc[g][:].bitcast(I32)[r:128:32, lo // 4 : hi // 4],
+                )
+
+        def o_group(g, h, eng_pieces):
+            og = work.tile([128, 512, 4], BF16, name="og", align_bytes=64)
+            ogs[g, h] = og
+            for n, eng in enumerate(eng_pieces):
+                wid = 512 // len(eng_pieces)
+                src = o_sb[g][:, :, 512 * h + wid * n : 512 * h + wid * (n + 1)].rearrange("p t f -> p f t")
+                dst = og[:, wid * n : wid * (n + 1), :]
+                if eng == "s":
+                    nc.scalar.copy(out=dst, in_=src)
+                else:
+                    nc.vector.tensor_copy(out=dst, in_=src)
+
+        def o_quant(g, h):
+            nc.vector.quantize_mx(
+                out=oq[g][:, 512 * h : 512 * (h + 1)].bitcast(FP8X4),
+                scales=osc[g][:, 512 * h : 512 * (h + 1)],
+                in_=ogs[g, h][:].rearrange("p n t -> p (n t)"),
+            )
+
+        def o_store(g, h, t, n=1):
+            cols = slice(512 * h, 512 * (h + 1))
+            nc.sync.dma_start(out=x_view(out_0, g)[:, t : t + n, cols], in_=o_sb[g][:, t : t + n, cols])
+
+        def q_store(g, h):
+            nc.sync.dma_start(
+                out=out_1[g].rearrange("p m t -> p (m t)").bitcast(I32)[:, 512 * h : 512 * (h + 1)],
+                in_=oq[g][:, 512 * h : 512 * (h + 1)].bitcast(I32),
+            )
+            for r in range(4):
+                nc.sync.dma_start(
+                    out=out_2[g].bitcast(I32).rearrange("(q r) n -> r q n", r=4)[r][:, 128 * h : 128 * (h + 1)],
+                    in_=osc[g][:].bitcast(I32)[r:128:32, 128 * h : 128 * (h + 1)],
+                )
+
+        x_transpose(0)
+        for q in range(2):
+            ap = ps_mm.tile([128, 512], F32, name="mm")
+            nc.tensor.matmul(ap[:], lhsT=ones[:], rhs=a_rows[:, q, 0:512], start=True, stop=True)
+            nc.vector.tensor_copy(out=a_bc[:, q, :], in_=ap[:])
+        acp = ps_mm.tile([128, 4, 2], F32, name="mm")
+        for n in range(4):
+            for q in range(2):
+                nc.tensor.matmul(
+                    acp[:, n, q : q + 1],
+                    lhsT=a_rows[:, q, 512 + 128 * n : 512 + 128 * (n + 1)],
+                    rhs=ones[:, 0:1],
+                    start=True,
+                    stop=True,
+                )
+        x_copy(0, "s")
+        x_quant(0)
+        nc.vector.tensor_copy(out=a_col[:], in_=acp[:])
+        x_transpose(1)
+        x_copy(1, "s")
+        x_quant(1)
+        nc.gpsimd.tensor_scalar(out=ri3[:], in0=ri_sb[:], scalar1=1.0 / EPS, scalar2=None, op0=MULT)
+        nc.gpsimd.tensor_copy(out=ro32[:], in_=ro_sb[:])
+        for s in range(8):
+            if s + 2 < 8:
+                x_transpose(s + 2)
+            zt_mm(s)
+            z_mm(s, 0)
+            if s > 0:
+                zt_score(s - 1)
+            if s >= 5:
+                adj_transpose(0, s - 5)
+                s_bcast(0, s - 5)
+            if s + 2 < 8:
+                x_copy(s + 2, "s")
+            zt_copy(s)
+            z_store(s, 0)
+            if s >= 5:
+                gate(0, s - 5)
+            z_score(s)
+            if s + 2 < 8:
+                x_quant(s + 2)
+            if s in (2, 4, 6):
+                score_sum(s // 2 - 1)
+            if s >= 6:
+                c_mul(0, s - 6)
+            if s == 3:
+                for c in range(2):
+                    zs_piece(0, 0, c)
+        zt_score(7)
+        z_mm(0, 1)
+        z_mm(1, 1)
+        adj_transpose(0, 3)
+        z_store(0, 1)
+        z_store(1, 1)
+        zs_piece(1, 0, 0)
+        c_quant(0, 0)
+        score_sum(3)
+        s_bcast(0, 3)
+        s_bcast(1, 0)
+        c_mul(0, 2)
+        c_quant(0, 1)
+        gate(0, 3)
+        adj_transpose(1, 0)
+        z_mm(2, 1)
+        z_mm(3, 1)
+        gate(1, 0)
+        zs_quant(0, 0)
+        c_mul(0, 3)
+        zs_piece(1, 0, 1, nc.vector)
+        s_bcast(1, 1)
+        adj_transpose(1, 1)
+        s_bcast(1, 2)
+        gate(1, 1)
+        z_store(2, 1)
+        z_store(3, 1)
+        for c in range(2):
+            zs_piece(0, 1, c)
+        c_quant(0, 2)
+        c_mul(1, 0)
+        adj_transpose(1, 2)
+        c_quant(0, 3)
+        gate(1, 2)
+        c_mul(1, 1)
+        s_bcast(1, 3)
+        adj_transpose(1, 3)
+        z_mm(4, 1)
+        z_mm(5, 1)
+        z_store(4, 1)
+        z_store(5, 1)
+        z_mm(6, 1)
+        z_mm(7, 1)
+        gate(1, 3)
+        c_quant(1, 0)
+        zs_quant(1, 0)
+        c_quant(1, 1)
+        z_store(6, 1)
+        z_store(7, 1)
+        for c in range(2):
+            zs_piece(1, 1, c)
+        units = [(g, h, t) for h in range(2) for g in range(2) for t in range(4)]
+        m_mm(*units[0])
+        m_mm(*units[1])
+        c_mul(1, 2)
+        pend = []
+        for n, (g, h, t) in enumerate(units[:12]):
+            if n == 2:
+                c_quant(1, 2)
+                c_mul(1, 3)
+            if n == 3:
+                c_quant(1, 3)
+            if n == 4:
+                zs_quant(0, 1)
+            if n == 6:
+                zs_quant(1, 1)
+            m_mm(*units[n + 2])
+            if n in OFFLOAD:
+                o_add_split(g, h, t)
+            else:
+                o_add(g, h, t)
+            if t == 3 and pend:
+                o_quant(*pend[0])
+                q_store(*pend[0])
+                pend.clear()
+            if t % 2 == 1:
+                o_store(g, h, t - 1, 2)
+            if t == 3:
+                o_group(g, h, "ss")
+                pend.append((g, h))
+        m_mm(1, 1, 2)
+        m_mm(1, 1, 3)
+        for t in range(4):
+            o_add_part(1, 1, t, 0)
+        o_quant(0, 1)
+        o_store_part(1, 1, 0)
+        code_store(0, 512, 1024)
+        scale_store(0, 512, 1024)
+        o_group_part(1, 1, 0, 0, 256, "s")
+        for t in range(4):
+            o_add_part(1, 1, t, 1)
+        o_store_part(1, 1, 1)
+        o_quant_part(1, 1, 0)
+        code_store(1, 512, 768)
+        o_group_part(1, 1, 1, 0, 128, "s")
+        o_group_part(1, 1, 1, 1, 128, "v")
+        o_quant_part(1, 1, 1)
+        code_store(1, 768, 1024)
+        scale_store(1, 512, 1024)

@@ -17,16 +17,237 @@ TANH = mybir.ActivationFunctionType.Tanh
 
 FLOPS = 2 * 1024 * 1024 * 1024 * 2
 EPS = 0.3
-OFFLOAD = ()
+ORDER = [
+    ("xT", (0,)),
+    ("xC", (0, "V")),
+    ("xT", (1,)),
+    ("xC", (1, "V")),
+    ("abc2", ()),
+    ("xQ", (0,)),
+    ("xT", (4,)),
+    ("xT", (2,)),
+    ("xC", (2, "V")),
+    ("zM", (0, 1)),
+    ("zM", (0, 0)),
+    ("xQ", (1,)),
+    ("xC", (4, "S")),
+    ("xQ", (2,)),
+    ("xT", (3,)),
+    ("zM", (1, 1)),
+    ("zSt", (0, 1, "S")),
+    ("xT", (7,)),
+    ("xC", (3, "S")),
+    ("zU", (0, 0, 0, "V")),
+    ("zM", (2, 0)),
+    ("zU", (0, 0, 1, "V")),
+    ("zSt", (1, 1, "S")),
+    ("xC", (7, "S")),
+    ("zSt", (0, 0, "S")),
+    ("xQ", (3,)),
+    ("zM", (3, 1)),
+    ("zU", (0, 1, 0, "G")),
+    ("xT", (6,)),
+    ("xQ", (4,)),
+    ("zU", (1, 1, 1, "V")),
+    ("zU", (2, 0, 0, "V")),
+    ("zU", (1, 1, 0, "V")),
+    ("zSt", (2, 0, "S")),
+    ("xQ", (7,)),
+    ("ri3", ()),
+    ("zU", (3, 1, 1, "V")),
+    ("xC", (6, "S")),
+    ("xT", (5,)),
+    ("xC", (5, "S")),
+    ("zM", (1, 0)),
+    ("zM", (3, 0)),
+    ("zU", (1, 0, 1, "V")),
+    ("aT", (0, 0)),
+    ("xQ", (6,)),
+    ("xQ", (5,)),
+    ("zSt", (3, 0, "S")),
+    ("zSt", (3, 1, "S")),
+    ("zSt", (1, 0, "V")),
+    ("zU", (1, 0, 0, "V")),
+    ("zT", (1, 2)),
+    ("zU", (3, 0, 1, "V")),
+    ("zU", (0, 1, 1, "G")),
+    ("sS2", (0,)),
+    ("zC", (1, 2, "S")),
+    ("zM", (2, 1)),
+    ("acp", ()),
+    ("zT", (1, 3)),
+    ("zU", (2, 0, 1, "G")),
+    ("zM", (5, 0)),
+    ("zU", (2, 1, 1, "V")),
+    ("zU", (3, 0, 0, "G")),
+    ("zU", (2, 1, 0, "V")),
+    ("zU", (3, 1, 0, "G")),
+    ("zC", (1, 3, "S")),
+    ("sB", (0,)),
+    ("zSt", (2, 1, "V")),
+    ("zSt", (5, 0, "V")),
+    ("zM", (4, 0)),
+    ("sS2", (1,)),
+    ("acol", ()),
+    ("zU", (5, 0, 0, "V")),
+    ("sC", (0, "S")),
+    ("zT", (1, 0)),
+    ("sB", (1,)),
+    ("zT", (1, 1)),
+    ("zs", (0, 1, 0, "V")),
+    ("zSt", (4, 0, "S")),
+    ("aT", (0, 1)),
+    ("zs", (0, 0, 1, "V")),
+    ("zM", (4, 1)),
+    ("zs", (0, 0, 0, "G")),
+    ("gt", (0, 0)),
+    ("zC", (1, 0, "S")),
+    ("zM", (7, 0)),
+    ("sC", (1, "S")),
+    ("cM", (0, 0)),
+    ("zC", (1, 1, "S")),
+    ("zM", (6, 0)),
+    ("zSt", (4, 1, "S")),
+    ("zSt", (7, 0, "S")),
+    ("zU", (6, 0, 0, "V")),
+    ("gt", (0, 1)),
+    ("zSt", (6, 0, "S")),
+    ("zS", (6,)),
+    ("zs", (0, 1, 1, "G")),
+    ("zM", (7, 1)),
+    ("zU", (4, 0, 0, "G")),
+    ("zM", (5, 1)),
+    ("zU", (4, 0, 1, "G")),
+    ("zSt", (5, 1, "S")),
+    ("zU", (7, 0, 0, "V")),
+    ("zS", (7,)),
+    ("zU", (7, 0, 1, "V")),
+    ("zU", (5, 0, 1, "G")),
+    ("cM", (0, 1)),
+    ("zS", (5,)),
+    ("zU", (6, 0, 1, "V")),
+    ("zS", (4,)),
+    ("cQ", (0, 1)),
+    ("zs", (1, 0, 0, "V")),
+    ("sS3", (3,)),
+    ("sS3", (2,)),
+    ("zSt", (7, 1, "S")),
+    ("zM", (6, 1)),
+    ("aT", (1, 0)),
+    ("zs", (1, 0, 1, "V")),
+    ("aT", (0, 2)),
+    ("zQ", (0, 0)),
+    ("zQ", (1, 0)),
+    ("zSt", (6, 1, "S")),
+    ("sB", (2,)),
+    ("gt", (1, 0)),
+    ("sC", (2, "S")),
+    ("zs", (1, 1, 0, "G")),
+    ("cM", (1, 0)),
+    ("cQ", (0, 0)),
+    ("cQ", (1, 0)),
+    ("gt", (0, 2)),
+    ("cM", (0, 2)),
+    ("aT", (1, 2)),
+    ("gt", (1, 2)),
+    ("mM", (0, 0, 0)),
+    ("aT", (1, 1)),
+    ("sB", (3,)),
+    ("mM", (0, 0, 1)),
+    ("cM", (1, 2)),
+    ("zs", (1, 1, 1, "G")),
+    ("cQ", (0, 2)),
+    ("gt", (1, 1)),
+    ("aT", (0, 3)),
+    ("sC", (3, "S")),
+    ("cQ", (1, 2)),
+    ("gt", (1, 3)),
+    ("oA", (0, 0, 1, "X")),
+    ("cM", (1, 1)),
+    ("mM", (1, 0, 1)),
+    ("oA", (0, 0, 0, "V")),
+    ("aT", (1, 3)),
+    ("cQ", (1, 1)),
+    ("zQ", (0, 1)),
+    ("gt", (0, 3)),
+    ("mM", (0, 0, 2)),
+    ("oA", (0, 0, 2, "X")),
+    ("mM", (0, 0, 3)),
+    ("oA", (0, 0, 3, "X")),
+    ("zQ", (1, 1)),
+    ("cM", (1, 3)),
+    ("mM", (1, 0, 0)),
+    ("oS", (0, 0, 0)),
+    ("oA", (1, 0, 1, "V")),
+    ("oA", (1, 0, 0, "V")),
+    ("mM", (0, 1, 1)),
+    ("cM", (0, 3)),
+    ("oA", (0, 1, 1, "V")),
+    ("mM", (0, 1, 3)),
+    ("mM", (0, 1, 2)),
+    ("mM", (0, 1, 0)),
+    ("cQ", (0, 3)),
+    ("cQ", (1, 3)),
+    ("oA", (0, 1, 2, "V")),
+    ("mM", (1, 0, 2)),
+    ("oA", (0, 1, 3, "X")),
+    ("mM", (1, 0, 3)),
+    ("oG", (0, 0, 0, "S")),
+    ("oA", (0, 1, 0, "V")),
+    ("mM", (1, 1, 3)),
+    ("oG", (0, 0, 1, "S")),
+    ("oA", (1, 0, 2, "V")),
+    ("mM", (1, 1, 0)),
+    ("oG", (0, 1, 1, "S")),
+    ("oA", (1, 0, 3, "V")),
+    ("oS", (1, 0, 0)),
+    ("oQ", (0, 0)),
+    ("oS", (0, 0, 2)),
+    ("oG", (0, 1, 0, "S")),
+    ("oS", (0, 1, 2)),
+    ("oS", (1, 0, 2)),
+    ("oP", (0, 0)),
+    ("mM", (1, 1, 2)),
+    ("mM", (1, 1, 1)),
+    ("oP", (0, 1)),
+    ("oP", (3, 0)),
+    ("oP", (2, 0)),
+    ("oP", (1, 1)),
+    ("qS", (0, 0)),
+    ("oQ", (0, 1)),
+    ("oP", (1, 0)),
+    ("oGp", (0, 0, "S")),
+    ("oG", (1, 0, 0, "S")),
+    ("oS", (0, 1, 0)),
+    ("oP", (2, 1)),
+    ("qS", (0, 1)),
+    ("oP", (3, 1)),
+    ("oSp", (0,)),
+    ("oGp", (1, 1, "V")),
+    ("oGp", (0, 1, "V")),
+    ("oGp", (1, 0, "V")),
+    ("oQp", (0,)),
+    ("oG", (1, 0, 1, "G")),
+    ("oQp", (1,)),
+    ("qSp", (0,)),
+    ("oQ", (1, 0)),
+    ("qSp", (1,)),
+    ("oSp", (1,)),
+    ("qS", (1, 0)),
+]
 
 
 def tile_fagcnsignedtanhpropagation_x2_kernel(tc, x, w_words, w_scales, adj, a1, a2, ri, ro, out_0, out_1, out_2):
     nc = tc.nc
     with ExitStack() as ctx:
         keep = ctx.enter_context(tc.tile_pool(name="keep", bufs=1))
+        zt_pool = ctx.enter_context(tc.tile_pool(name="zt_pool", bufs=4))
+        wide = ctx.enter_context(tc.tile_pool(name="wide", bufs=3))
+        wide4 = ctx.enter_context(tc.tile_pool(name="wide4", bufs=4))
         work = ctx.enter_context(tc.tile_pool(name="work", bufs=2))
         ps_tr = ctx.enter_context(tc.psum_pool(name="ps_tr", bufs=2))
         ps_mm = ctx.enter_context(tc.psum_pool(name="ps_mm", bufs=4))
+        ps_c = ctx.enter_context(tc.psum_pool(name="ps_c", bufs=1))
         ps_s = ctx.enter_context(tc.psum_pool(name="ps_s", bufs=1))
         ctx.enter_context(tc.manual_schedule())
 
@@ -35,7 +256,7 @@ def tile_fagcnsignedtanhpropagation_x2_kernel(tc, x, w_words, w_scales, adj, a1,
         w_codes = keep.tile([128, 2, 2048], U8, name="w_codes", align_bytes=64)
         w_sc = keep.tile([128, 2, 1024], U8, name="w_sc", align_bytes=64)
         a_rows = keep.tile([128, 2, 1024], BF16, name="a_rows", align_bytes=64)
-        a_bc = keep.tile([128, 2, 512], BF16, name="a_bc", align_bytes=64)
+        a_bc = keep.tile([128, 2, 1024], BF16, name="a_bc", align_bytes=64)
         a_col = keep.tile([128, 4, 2], F32, name="a_col", align_bytes=64)
         ones = keep.tile([128, 128], BF16, name="ones", align_bytes=64)
         ident = keep.tile([128, 128], F32, name="ident", align_bytes=64)
@@ -44,11 +265,12 @@ def tile_fagcnsignedtanhpropagation_x2_kernel(tc, x, w_words, w_scales, adj, a1,
         ro32 = keep.tile([128, 2, 4], F32, name="ro32")
         ri3 = keep.tile([128, 2, 4], F32, name="ri3")
         dummy = keep.tile([128, 1], F32, name="dummy")
-        part = [keep.tile([128, 4, 2], F32, name=f"part{g}") for g in range(2)]
+        part = [keep.tile([128, 4, 2, 2], F32, name=f"part{g}") for g in range(2)]
+        s_row = keep.tile([128, 1024], F32, name="s_row", align_bytes=64)
         score = [keep.tile([128, 4, 2], F32, name=f"score{g}") for g in range(2)]
         z03 = [keep.tile([128, 4, 1024], F32, name=f"z03_{g}", align_bytes=64) for g in range(2)]
-        xq = [keep.tile([128, 2, 128], U32, name=f"xq{s}", align_bytes=64) for s in range(8)]
-        xs = [keep.tile([128, 2, 128], U8, name=f"xs{s}", align_bytes=64) for s in range(8)]
+        xq = [keep.tile([128, 2, 512], U32, name=f"xq{g}", align_bytes=64) for g in range(2)]
+        xs = [keep.tile([128, 2, 512], U8, name=f"xs{g}", align_bytes=64) for g in range(2)]
         zq = [keep.tile([128, 1024], U32, name=f"zq{g}", align_bytes=64) for g in range(2)]
         zsc = [keep.tile([128, 1024], U8, name=f"zsc{g}", align_bytes=64) for g in range(2)]
         cq = [[keep.tile([128, 512], U32, name=f"cq{j}{i}", align_bytes=64) for i in range(2)] for j in range(2)]
@@ -57,10 +279,10 @@ def tile_fagcnsignedtanhpropagation_x2_kernel(tc, x, w_words, w_scales, adj, a1,
         oq = [keep.tile([128, 1024], U32, name=f"oq{g}", align_bytes=64) for g in range(2)]
         osc = [keep.tile([128, 1024], U8, name=f"osc{g}", align_bytes=64) for g in range(2)]
 
+        nc.gpsimd.memset(dummy[:], 0.0)
+        nc.vector.memset(w_sc[:].bitcast(I32), 0)
         nc.vector.memset(a_rows[:], 0.0)
-        nc.gpsimd.memset(w_sc[:].bitcast(I32), 0)
         nc.vector.memset(ones[:], 1.0)
-        nc.vector.memset(dummy[:], 0.0)
         make_identity(nc, ident[:])
 
         def x_view(t_dram, g):
@@ -71,18 +293,21 @@ def tile_fagcnsignedtanhpropagation_x2_kernel(tc, x, w_words, w_scales, adj, a1,
             nc.sync.dma_start(out=x_sb[g][:, t : t + n, :], in_=x_view(x, g)[:, t : t + n, :])
 
         load_x(0)
-        for g in range(2):
-            nc.sync.dma_start(out=w_codes[:].bitcast(I32)[:, g, 0:256], in_=w_words.bitcast(I32)[g][:, 0:256])
-        load_x(1)
-        for g in range(2):
-            nc.sync.dma_start(out=w_codes[:].bitcast(I32)[:, g, 256:512], in_=w_words.bitcast(I32)[g][:, 256:512])
         for r in range(4):
-            nc.scalar.dma_start(
+            nc.sync.dma_start(
                 out=w_sc[:].bitcast(I32)[r:128:32, :, :],
                 in_=w_scales.bitcast(I32).rearrange("g (q r) n -> r q g n", r=4)[r],
             )
-        nc.scalar.dma_start(out=a_rows[0:1, 0, :], in_=a1.unsqueeze(0))
-        nc.scalar.dma_start(out=a_rows[0:1, 1, :], in_=a2.unsqueeze(0))
+        for h in range(2):
+            for g in range(2):
+                nc.sync.dma_start(
+                    out=w_codes[:].bitcast(I32)[:, g, 256 * h : 256 * (h + 1)],
+                    in_=w_words.bitcast(I32)[g][:, 256 * h : 256 * (h + 1)],
+                )
+            if h == 0:
+                nc.sync.dma_start(out=a_rows[0:1, 0, :], in_=a1.unsqueeze(0))
+                nc.sync.dma_start(out=a_rows[0:1, 1, :], in_=a2.unsqueeze(0))
+                load_x(1)
         nc.scalar.activation(out=dummy[:], in_=dummy[:], func=TANH)
         load_x(2, 2)
         load_x(4, 2)
@@ -107,30 +332,31 @@ def tile_fagcnsignedtanhpropagation_x2_kernel(tc, x, w_words, w_scales, adj, a1,
                     nc.tensor.transpose(tr[:, k, u, :], words[:, 256 * k + u : 256 * (k + 1) : 2], ident[:])
             trs[s] = tr
 
-        def x_copy(s, eng):
-            xg = work.tile([128, 2, 128, 4], BF16, name="xg", align_bytes=64)
+        def x_copy(s, eng="S"):
+            xg = wide.tile([128, 2, 128, 4], BF16, name="xg", align_bytes=64)
             dst = xg[:].rearrange("p k r t -> p (k r t)").bitcast(F32).rearrange("p (k r u) -> p k r u", k=2, u=2)
             src = trs[s][:].rearrange("p k u r -> p k r u")
-            if eng == "s":
+            if eng == "S":
                 nc.scalar.copy(out=dst, in_=src)
             else:
                 nc.vector.tensor_copy(out=dst, in_=src)
             grp[s] = xg
 
         def x_quant(s):
-            nc.vector.quantize_mx(
-                out=xq[s][:].rearrange("p k r -> p (k r)").bitcast(FP8X4),
-                scales=xs[s][:].rearrange("p k r -> p (k r)"),
-                in_=grp[s][:].rearrange("p k r t -> p (k r t)"),
-            )
+            for k in range(2):
+                nc.vector.quantize_mx(
+                    out=xq[s // 4][:, k, 128 * (s % 4) : 128 * (s % 4 + 1)].bitcast(FP8X4),
+                    scales=xs[s // 4][:, k, 128 * (s % 4) : 128 * (s % 4 + 1)],
+                    in_=grp[s][:, k, :, :].rearrange("p r t -> p (r t)"),
+                )
 
         def z_mm(s, h):
             zp = ps_mm.tile([128, 512], F32, name="mm")
             for k in range(2):
                 nc.tensor.matmul_mx(
                     out=zp[:],
-                    lhsT=xq[s][:, k, :].bitcast(FP8X4),
-                    lhsT_scale=xs[s][:, k, :],
+                    lhsT=xq[s // 4][:, k, 128 * (s % 4) : 128 * (s % 4 + 1)].bitcast(FP8X4),
+                    lhsT_scale=xs[s // 4][:, k, 128 * (s % 4) : 128 * (s % 4 + 1)],
                     rhs=w_codes[:, k, 1024 * h : 1024 * (h + 1)].bitcast(FP4X4),
                     rhs_scale=w_sc[:, k, 512 * h : 512 * (h + 1)],
                     start=(k == 0),
@@ -138,87 +364,120 @@ def tile_fagcnsignedtanhpropagation_x2_kernel(tc, x, w_words, w_scales, adj, a1,
                 )
             zps[s, h] = zp
 
-        def zt_mm(s):
-            zp = ps_mm.tile([128, 4, 128], F32, name="mm")
-            for n in range(4):
-                for k in range(2):
-                    nc.tensor.matmul_mx(
-                        out=zp[:, n, :],
-                        lhsT=w_codes[:, k, 1024 + 256 * n : 1024 + 256 * (n + 1)].bitcast(FP4X4),
-                        lhsT_scale=w_sc[:, k, 512 + 128 * n : 512 + 128 * (n + 1)],
-                        rhs=xq[s][:, k, :].bitcast(FP8X4),
-                        rhs_scale=xs[s][:, k, :],
-                        start=(k == 0),
-                        stop=(k == 1),
-                    )
-            zps[s, "t"] = zp
+        sc = ps_c.tile([128, 4, 2], F32, name="sc")
+        zts = {}
 
-        def zt_copy(s):
-            zt = work.tile([128, 4, 128], F32, name="zt", align_bytes=64)
-            nc.scalar.copy(out=zt[:], in_=zps[s, "t"][:])
-            zts[s] = zt
+        def zt_mm(g, n):
+            zp = ps_mm.tile([128, 512], F32, name="mm")
+            for k in range(2):
+                nc.tensor.matmul_mx(
+                    out=zp[:],
+                    lhsT=w_codes[:, k, 1024 + 256 * n : 1024 + 256 * (n + 1)].bitcast(FP4X4),
+                    lhsT_scale=w_sc[:, k, 512 + 128 * n : 512 + 128 * (n + 1)],
+                    rhs=xq[g][:, k, :].bitcast(FP8X4),
+                    rhs_scale=xs[g][:, k, :],
+                    start=(k == 0),
+                    stop=(k == 1),
+                )
+            zps[g, n, "t"] = zp
 
-        sp = [ps_s.tile([128, 512], F32, name=f"sp{g}") for g in range(2)]
-        sc = [sp[g][:, 256:264].rearrange("p (t q) -> p t q", q=2) for g in range(2)]
+        def zt_copy(g, n, eng="S"):
+            zt = zt_pool.tile([128, 512], F32, name="zt", align_bytes=64)
+            if eng == "S":
+                nc.scalar.copy(out=zt[:], in_=zps[g, n, "t"][:])
+            else:
+                nc.vector.tensor_copy(out=zt[:], in_=zps[g, n, "t"][:])
+            zts[g, n] = zt
 
         def zt_score(s):
+            g, t = s // 4, s % 4
             for n in range(4):
-                nc.tensor.matmul(sc[s // 4][:, s % 4, :], lhsT=zts[s][:, n, :], rhs=a_col[:, n, :], start=(n == 0), stop=(n == 3))
+                nc.tensor.matmul(
+                    sc[:, t, :], lhsT=zts[g, n][:, 128 * t : 128 * (t + 1)], rhs=a_col[:, n, :], start=(n == 0), stop=(n == 3)
+                )
 
-        def z_store(s, h):
+        def z_store(s, h, eng="S"):
             g, t = s // 4, s % 4
-            nc.scalar.activation(out=z03[g][:, t, 512 * h : 512 * (h + 1)], in_=zps[s, h][:], func=COPY, scale=EPS)
+            dst = z03[g][:, t, 512 * h : 512 * (h + 1)]
+            if eng == "S":
+                nc.scalar.activation(out=dst, in_=zps[s, h][:], func=COPY, scale=EPS)
+            else:
+                nc.vector.tensor_scalar(out=dst, in0=zps[s, h][:], scalar1=EPS, scalar2=None, op0=MULT)
 
-        def z_score(s):
+        def unit_cols(h):
+            return slice(512 * h, 512 * (h + 1))
+
+        def score_unit(s, h, q, eng="V"):
             g, t = s // 4, s % 4
-            for q in (1, 0):
+            acc = part[g][:, t, q, h : h + 1]
+            if eng == "V":
                 junk = work.tile([128, 512], F32, name="junk")
                 nc.vector.scalar_tensor_tensor(
                     out=junk[:],
-                    in0=zps[s, 0][:],
+                    in0=zps[s, h][:],
                     scalar=1.0,
-                    in1=a_bc[:, q, :],
+                    in1=a_bc[:, q, unit_cols(h)],
                     op0=MULT,
                     op1=MULT,
-                    accum_out=part[g][:, t, q : q + 1],
+                    accum_out=acc,
                 )
+            else:
+                pr = wide.tile([128, 512], F32, name="pr")
+                nc.gpsimd.tensor_tensor(out=pr[:], in0=z03[g][:, t, unit_cols(h)], in1=a_bc[:, q, unit_cols(h)], op=MULT)
+                jk = work.tile([128, 512], F32, name="jk")
+                nc.scalar.activation(out=jk[:], in_=pr[:], func=COPY, scale=1.0 / EPS, accum_out=acc)
 
-        def score_sum(n):
+        def score_sum_units(n):
             g, ts = n // 2, slice(2 * (n % 2), 2 * (n % 2) + 2)
-            nc.vector.tensor_tensor(out=score[g][:, ts, :], in0=sc[g][:, ts, :], in1=part[g][:, ts, :], op=ADD)
+            nc.vector.tensor_reduce(out=score[g][:, ts, :], in_=part[g][:, ts, :, :], axis=mybir.AxisListType.X, op=ADD)
+
+        def score_sum_psum(n):
+            g, ts = n // 2, slice(2 * (n % 2), 2 * (n % 2) + 2)
+            nc.vector.tensor_tensor(out=score[g][:, ts, :], in0=sc[:, ts, :], in1=part[g][:, ts, :, 0], op=ADD)
 
         gates = {}
-        bcast_count = [0]
+        sps = {}
 
-        def s_bcast(j, n):
-            bank = sp[bcast_count[0] % 2]
-            bcast_count[0] += 1
+        def s_bcast(n):
+            bank = ps_s.tile([128, 256], F32, name="sp")
             for b in range(2):
                 nc.tensor.transpose(
                     bank[:, 128 * b : 128 * (b + 1)],
                     score[n // 2][:, 2 * (n % 2) + b, 0:1].to_broadcast([128, 128]),
                     ident[:],
                 )
-            gates[j, n] = bank
+            sps[n] = bank
+
+        def s_copy(n, eng="S"):
+            dst = s_row[:, 256 * n : 256 * (n + 1)]
+            if eng == "S":
+                nc.scalar.copy(out=dst, in_=sps[n][:])
+            else:
+                nc.vector.tensor_copy(out=dst, in_=sps[n][:])
 
         def gate(j, n):
-            gt = work.tile([128, 4, 256], F32, name="gate", align_bytes=64)
+            gt = wide.tile([128, 4, 256], F32, name="gate", align_bytes=64)
             for t in range(4):
-                nc.scalar.activation(out=gt[:, t, :], in_=gates[j, n][:, 0:256], func=TANH, bias=score[j][:, t, 1:2])
+                nc.scalar.activation(
+                    out=gt[:, t, :], in_=s_row[:, 256 * n : 256 * (n + 1)], func=TANH, bias=score[j][:, t, 1:2]
+                )
             gates[j, n] = gt
 
         zgt = {}
 
-        def zs_piece(g, h, c, eng=nc.gpsimd):
-            if c == 0:
-                zgt[g, h] = work.tile([128, 512, 4], BF16, name="zg", align_bytes=64)
-            cols = slice(512 * h + 256 * c, 512 * h + 256 * (c + 1))
-            eng.tensor_tensor(
-                out=zgt[g, h][:, 256 * c : 256 * (c + 1), :],
-                in0=z03[g][:, :, cols].rearrange("p t f -> p f t"),
-                in1=ri3[:, g, :].unsqueeze(1).to_broadcast([128, 256, 4]),
-                op=MULT,
-            )
+        def zs_piece(g, h, c, eng="V"):
+            if (g, h) not in zgt:
+                zgt[g, h] = wide4.tile([128, 512, 4], BF16, name="zg", align_bytes=64)
+            parts, on = (1, nc.vector) if eng == "V" else (2, nc.gpsimd)
+            wid = 256 // parts
+            for n in range(parts):
+                lo = 256 * c + wid * n
+                on.tensor_tensor(
+                    out=zgt[g, h][:, lo : lo + wid, :],
+                    in0=z03[g][:, :, 512 * h + lo : 512 * h + lo + wid].rearrange("p t f -> p f t"),
+                    in1=ri3[:, g, :].unsqueeze(1).to_broadcast([128, wid, 4]),
+                    op=MULT,
+                )
 
         def zs_quant(g, h):
             nc.vector.quantize_mx(
@@ -238,7 +497,7 @@ def tile_fagcnsignedtanhpropagation_x2_kernel(tc, x, w_words, w_scales, adj, a1,
         cgs = {}
 
         def c_mul(j, n):
-            cg = work.tile([128, 256, 4], BF16, name="cg", align_bytes=64)
+            cg = wide.tile([128, 256, 4], BF16, name="cg", align_bytes=64)
             nc.vector.tensor_tensor(
                 out=cg[:].rearrange("p n (u e) -> p n u e", u=2),
                 in0=trs[j, n][:].rearrange("p u n -> p (u n)").bitcast(BF16).rearrange("p (u n e) -> p n u e", u=2, e=2),
@@ -271,60 +530,74 @@ def tile_fagcnsignedtanhpropagation_x2_kernel(tc, x, w_words, w_scales, adj, a1,
                 )
             mps[g, h, t] = mp
 
-        def o_add(g, h, t):
+        def o_add(g, h, t, eng="V"):
             cols = slice(512 * h, 512 * (h + 1))
-            nc.vector.scalar_tensor_tensor(
-                out=o_sb[g][:, t, cols],
-                in0=mps[g, h, t][:],
-                scalar=ro_sb[:, g, t : t + 1],
-                in1=z03[g][:, t, cols],
-                op0=MULT,
-                op1=ADD,
-            )
+            if eng == "V":
+                nc.vector.scalar_tensor_tensor(
+                    out=o_sb[g][:, t, cols],
+                    in0=mps[g, h, t][:],
+                    scalar=ro_sb[:, g, t : t + 1],
+                    in1=z03[g][:, t, cols],
+                    op0=MULT,
+                    op1=ADD,
+                )
+            else:
+                mr = wide.tile([128, 512], F32, name="mr", align_bytes=64)
+                nc.scalar.activation(out=mr[:], in_=mps[g, h, t][:], func=COPY, scale=ro32[:, g, t : t + 1])
+                nc.gpsimd.tensor_tensor(out=o_sb[g][:, t, cols], in0=mr[:], in1=z03[g][:, t, cols], op=ADD)
 
-        def o_add_split(g, h, t):
-            cols = slice(512 * h, 512 * (h + 1))
-            mr = work.tile([128, 512], F32, name="mr", align_bytes=64)
-            nc.scalar.activation(out=mr[:], in_=mps[g, h, t][:], func=COPY, scale=ro32[:, g, t : t + 1])
-            nc.gpsimd.tensor_tensor(out=o_sb[g][:, t, cols], in0=mr[:], in1=z03[g][:, t, cols], op=ADD)
-
-        def o_add_part(g, h, t, c):
-            cols = slice(512 * h + 256 * c, 512 * h + 256 * (c + 1))
+        def o_add_part(t, c):
+            cols = slice(512 + 256 * c, 512 + 256 * (c + 1))
             nc.vector.scalar_tensor_tensor(
-                out=o_sb[g][:, t, cols],
-                in0=mps[g, h, t][:, 256 * c : 256 * (c + 1)],
-                scalar=ro_sb[:, g, t : t + 1],
-                in1=z03[g][:, t, cols],
+                out=o_sb[1][:, t, cols],
+                in0=mps[1, 1, t][:, 256 * c : 256 * (c + 1)],
+                scalar=ro_sb[:, 1, t : t + 1],
+                in1=z03[1][:, t, cols],
                 op0=MULT,
                 op1=ADD,
             )
 
         ogs = {}
 
-        def o_group_part(g, h, c, n, wid, eng):
+        def o_group_cols(g, h, lo, wid, eng):
             if (g, h) not in ogs:
-                ogs[g, h] = work.tile([128, 512, 4], BF16, name="og", align_bytes=64)
-            lo = 256 * c + wid * n
+                ogs[g, h] = wide.tile([128, 512, 4], BF16, name="og", align_bytes=64)
             src = o_sb[g][:, :, 512 * h + lo : 512 * h + lo + wid].rearrange("p t f -> p f t")
             dst = ogs[g, h][:, lo : lo + wid, :]
-            if eng == "s":
+            if eng == "S":
                 nc.scalar.copy(out=dst, in_=src)
-            elif eng == "g":
-                nc.gpsimd.tensor_scalar(out=dst, in0=src, scalar1=1.0, scalar2=0.0, op0=MULT, op1=ADD)
-            else:
+            elif eng == "V":
                 nc.vector.tensor_copy(out=dst, in_=src)
+            else:
+                nc.gpsimd.tensor_scalar(out=dst, in0=src, scalar1=1.0, scalar2=0.0, op0=MULT, op1=ADD)
 
-        def o_quant_part(g, h, c):
-            cols = slice(512 * h + 256 * c, 512 * h + 256 * (c + 1))
+        def o_group(g, h, c, eng="S"):
+            o_group_cols(g, h, 256 * c, 256, eng)
+
+        def o_group_part(c, n, eng="S"):
+            o_group_cols(1, 1, 256 * c + 128 * n, 128, eng)
+
+        def o_quant_cols(g, h, lo, wid):
+            cols = slice(512 * h + lo, 512 * h + lo + wid)
             nc.vector.quantize_mx(
                 out=oq[g][:, cols].bitcast(FP8X4),
                 scales=osc[g][:, cols],
-                in_=ogs[g, h][:, 256 * c : 256 * (c + 1), :].rearrange("p n t -> p (n t)"),
+                in_=ogs[g, h][:, lo : lo + wid, :].rearrange("p n t -> p (n t)"),
             )
 
-        def o_store_part(g, h, c):
-            cols = slice(512 * h + 256 * c, 512 * h + 256 * (c + 1))
-            nc.sync.dma_start(out=x_view(out_0, g)[:, :, cols], in_=o_sb[g][:, :, cols])
+        def o_quant(g, h):
+            o_quant_cols(g, h, 0, 512)
+
+        def o_quant_part(c):
+            o_quant_cols(1, 1, 256 * c, 256)
+
+        def o_store(g, h, t):
+            cols = slice(512 * h, 512 * (h + 1))
+            nc.sync.dma_start(out=x_view(out_0, g)[:, t : t + 2, cols], in_=o_sb[g][:, t : t + 2, cols])
+
+        def o_store_part(c):
+            cols = slice(512 + 256 * c, 512 + 256 * (c + 1))
+            nc.sync.dma_start(out=x_view(out_0, 1)[:, :, cols], in_=o_sb[1][:, :, cols])
 
         def code_store(g, lo, hi):
             nc.sync.dma_start(
@@ -339,185 +612,56 @@ def tile_fagcnsignedtanhpropagation_x2_kernel(tc, x, w_words, w_scales, adj, a1,
                     in_=osc[g][:].bitcast(I32)[r:128:32, lo // 4 : hi // 4],
                 )
 
-        def o_group(g, h, eng_pieces):
-            og = work.tile([128, 512, 4], BF16, name="og", align_bytes=64)
-            ogs[g, h] = og
-            for n, eng in enumerate(eng_pieces):
-                wid = 512 // len(eng_pieces)
-                src = o_sb[g][:, :, 512 * h + wid * n : 512 * h + wid * (n + 1)].rearrange("p t f -> p f t")
-                dst = og[:, wid * n : wid * (n + 1), :]
-                if eng == "s":
-                    nc.scalar.copy(out=dst, in_=src)
-                else:
-                    nc.vector.tensor_copy(out=dst, in_=src)
-
-        def o_quant(g, h):
-            nc.vector.quantize_mx(
-                out=oq[g][:, 512 * h : 512 * (h + 1)].bitcast(FP8X4),
-                scales=osc[g][:, 512 * h : 512 * (h + 1)],
-                in_=ogs[g, h][:].rearrange("p n t -> p (n t)"),
-            )
-
-        def o_store(g, h, t, n=1):
-            cols = slice(512 * h, 512 * (h + 1))
-            nc.sync.dma_start(out=x_view(out_0, g)[:, t : t + n, cols], in_=o_sb[g][:, t : t + n, cols])
-
         def q_store(g, h):
-            nc.sync.dma_start(
-                out=out_1[g].rearrange("p m t -> p (m t)").bitcast(I32)[:, 512 * h : 512 * (h + 1)],
-                in_=oq[g][:, 512 * h : 512 * (h + 1)].bitcast(I32),
-            )
-            for r in range(4):
-                nc.sync.dma_start(
-                    out=out_2[g].bitcast(I32).rearrange("(q r) n -> r q n", r=4)[r][:, 128 * h : 128 * (h + 1)],
-                    in_=osc[g][:].bitcast(I32)[r:128:32, 128 * h : 128 * (h + 1)],
-                )
+            code_store(g, 512 * h, 512 * (h + 1))
+            scale_store(g, 512 * h, 512 * (h + 1))
 
-        x_transpose(0)
-        for q in range(2):
-            ap = ps_mm.tile([128, 512], F32, name="mm")
-            nc.tensor.matmul(ap[:], lhsT=ones[:], rhs=a_rows[:, q, 0:512], start=True, stop=True)
-            nc.vector.tensor_copy(out=a_bc[:, q, :], in_=ap[:])
-        acp = ps_mm.tile([128, 4, 2], F32, name="mm")
-        for n in range(4):
+        def q_store_part(c):
+            code_store(1, 512 + 256 * c, 512 + 256 * (c + 1))
+            if c == 1:
+                scale_store(1, 512, 1024)
+
+        def a_rows_to_all():
             for q in range(2):
-                nc.tensor.matmul(
-                    acp[:, n, q : q + 1],
-                    lhsT=a_rows[:, q, 512 + 128 * n : 512 + 128 * (n + 1)],
-                    rhs=ones[:, 0:1],
-                    start=True,
-                    stop=True,
-                )
-        x_copy(0, "s")
-        x_quant(0)
-        nc.vector.tensor_copy(out=a_col[:], in_=acp[:])
-        x_transpose(1)
-        x_copy(1, "s")
-        x_quant(1)
-        nc.gpsimd.tensor_scalar(out=ri3[:], in0=ri_sb[:], scalar1=1.0 / EPS, scalar2=None, op0=MULT)
-        nc.gpsimd.tensor_copy(out=ro32[:], in_=ro_sb[:])
-        for s in range(8):
-            if s + 2 < 8:
-                x_transpose(s + 2)
-            zt_mm(s)
-            z_mm(s, 0)
-            if s > 0:
-                zt_score(s - 1)
-            if s >= 5:
-                adj_transpose(0, s - 5)
-                s_bcast(0, s - 5)
-            if s + 2 < 8:
-                x_copy(s + 2, "s")
-            zt_copy(s)
-            z_store(s, 0)
-            if s >= 5:
-                gate(0, s - 5)
-            z_score(s)
-            if s + 2 < 8:
-                x_quant(s + 2)
-            if s in (2, 4, 6):
-                score_sum(s // 2 - 1)
-            if s >= 6:
-                c_mul(0, s - 6)
-            if s == 3:
-                for c in range(2):
-                    zs_piece(0, 0, c)
-        zt_score(7)
-        z_mm(0, 1)
-        z_mm(1, 1)
-        adj_transpose(0, 3)
-        z_store(0, 1)
-        z_store(1, 1)
-        zs_piece(1, 0, 0)
-        c_quant(0, 0)
-        score_sum(3)
-        s_bcast(0, 3)
-        s_bcast(1, 0)
-        c_mul(0, 2)
-        c_quant(0, 1)
-        gate(0, 3)
-        adj_transpose(1, 0)
-        z_mm(2, 1)
-        z_mm(3, 1)
-        gate(1, 0)
-        zs_quant(0, 0)
-        c_mul(0, 3)
-        zs_piece(1, 0, 1, nc.vector)
-        s_bcast(1, 1)
-        adj_transpose(1, 1)
-        s_bcast(1, 2)
-        gate(1, 1)
-        z_store(2, 1)
-        z_store(3, 1)
-        for c in range(2):
-            zs_piece(0, 1, c)
-        c_quant(0, 2)
-        c_mul(1, 0)
-        adj_transpose(1, 2)
-        c_quant(0, 3)
-        gate(1, 2)
-        c_mul(1, 1)
-        s_bcast(1, 3)
-        adj_transpose(1, 3)
-        z_mm(4, 1)
-        z_mm(5, 1)
-        z_store(4, 1)
-        z_store(5, 1)
-        z_mm(6, 1)
-        z_mm(7, 1)
-        gate(1, 3)
-        c_quant(1, 0)
-        zs_quant(1, 0)
-        c_quant(1, 1)
-        z_store(6, 1)
-        z_store(7, 1)
-        for c in range(2):
-            zs_piece(1, 1, c)
-        units = [(g, h, t) for h in range(2) for g in range(2) for t in range(4)]
-        m_mm(*units[0])
-        m_mm(*units[1])
-        c_mul(1, 2)
-        pend = []
-        for n, (g, h, t) in enumerate(units[:12]):
-            if n == 2:
-                c_quant(1, 2)
-                c_mul(1, 3)
-            if n == 3:
-                c_quant(1, 3)
-            if n == 4:
-                zs_quant(0, 1)
-            if n == 6:
-                zs_quant(1, 1)
-            m_mm(*units[n + 2])
-            if n in OFFLOAD:
-                o_add_split(g, h, t)
-            else:
-                o_add(g, h, t)
-            if t == 3 and pend:
-                o_quant(*pend[0])
-                q_store(*pend[0])
-                pend.clear()
-            if t % 2 == 1:
-                o_store(g, h, t - 1, 2)
-            if t == 3:
-                o_group(g, h, "ss")
-                pend.append((g, h))
-        m_mm(1, 1, 2)
-        m_mm(1, 1, 3)
-        for t in range(4):
-            o_add_part(1, 1, t, 0)
-        o_quant(0, 1)
-        o_store_part(1, 1, 0)
-        code_store(0, 512, 1024)
-        scale_store(0, 512, 1024)
-        o_group_part(1, 1, 0, 0, 256, "s")
-        for t in range(4):
-            o_add_part(1, 1, t, 1)
-        o_store_part(1, 1, 1)
-        o_quant_part(1, 1, 0)
-        code_store(1, 512, 768)
-        o_group_part(1, 1, 1, 0, 128, "s")
-        o_group_part(1, 1, 1, 1, 128, "v")
-        o_quant_part(1, 1, 1)
-        code_store(1, 768, 1024)
-        scale_store(1, 512, 1024)
+                for h in range(2):
+                    ap = ps_mm.tile([128, 512], F32, name="mm")
+                    nc.tensor.matmul(ap[:], lhsT=ones[:], rhs=a_rows[:, q, 512 * h : 512 * (h + 1)], start=True, stop=True)
+                    dst = a_bc[:, q, 512 * h : 512 * (h + 1)]
+                    if h == 0:
+                        nc.vector.tensor_copy(out=dst, in_=ap[:])
+                    else:
+                        nc.scalar.copy(out=dst, in_=ap[:])
+
+        acps = {}
+
+        def a_to_columns():
+            acp = ps_mm.tile([128, 4, 2], F32, name="mm")
+            for n in range(4):
+                for q in range(2):
+                    nc.tensor.matmul(
+                        acp[:, n, q : q + 1],
+                        lhsT=a_rows[:, q, 512 + 128 * n : 512 + 128 * (n + 1)],
+                        rhs=ones[:, 0:1],
+                        start=True,
+                        stop=True,
+                    )
+            acps[0] = acp
+
+        def a_columns_copy():
+            nc.vector.tensor_copy(out=a_col[:], in_=acps[0][:])
+
+        def node_scales():
+            nc.gpsimd.tensor_scalar(out=ri3[:], in0=ri_sb[:], scalar1=1.0 / EPS, scalar2=None, op0=MULT)
+            nc.gpsimd.tensor_copy(out=ro32[:], in_=ro_sb[:])
+
+        steps = {
+            "abc2": a_rows_to_all, "acp": a_to_columns, "acol": a_columns_copy, "ri3": node_scales,
+            "xT": x_transpose, "xC": x_copy, "xQ": x_quant, "zM": z_mm, "zU": score_unit, "zSt": z_store,
+            "zT": zt_mm, "zC": zt_copy, "zS": zt_score, "sS2": score_sum_units, "sS3": score_sum_psum,
+            "sB": s_bcast, "sC": s_copy, "gt": gate, "aT": adj_transpose, "cM": c_mul, "cQ": c_quant,
+            "zs": zs_piece, "zQ": zs_quant, "mM": m_mm, "oA": o_add, "oP": o_add_part, "oG": o_group,
+            "oGp": o_group_part, "oQ": o_quant, "oQp": o_quant_part, "oS": o_store, "oSp": o_store_part,
+            "qS": q_store, "qSp": q_store_part,
+        }
+        for name, args in ORDER:
+            steps[name](*args)

from contextlib import ExitStack

import concourse.mybir as mybir
from concourse.masks import make_identity

F32 = mybir.dt.float32
BF16 = mybir.dt.bfloat16
I32 = mybir.dt.int32
U32 = mybir.dt.uint32
U8 = mybir.dt.uint8
FP8X4 = mybir.dt.float8_e4m3fn_x4
FP4X4 = mybir.dt.float4_e2m1fn_x4
MULT = mybir.AluOpType.mult
ADD = mybir.AluOpType.add
COPY = mybir.ActivationFunctionType.Copy
TANH = mybir.ActivationFunctionType.Tanh

FLOPS = 2 * 1024 * 1024 * 1024 * 2
EPS = 0.3
ORDER = [
    ("xT", (0,)),
    ("xC", (0, "V")),
    ("xT", (1,)),
    ("xC", (1, "V")),
    ("abc2", ()),
    ("xQ", (0,)),
    ("xT", (4,)),
    ("xT", (2,)),
    ("xC", (2, "V")),
    ("zM", (0, 1)),
    ("zM", (0, 0)),
    ("xQ", (1,)),
    ("xC", (4, "S")),
    ("xQ", (2,)),
    ("xT", (3,)),
    ("zM", (1, 1)),
    ("zSt", (0, 1, "S")),
    ("xT", (7,)),
    ("xC", (3, "S")),
    ("zU", (0, 0, 0, "V")),
    ("zM", (2, 0)),
    ("zU", (0, 0, 1, "V")),
    ("zSt", (1, 1, "S")),
    ("xC", (7, "S")),
    ("zSt", (0, 0, "S")),
    ("xQ", (3,)),
    ("zM", (3, 1)),
    ("zU", (0, 1, 0, "G")),
    ("xT", (6,)),
    ("xQ", (4,)),
    ("zU", (1, 1, 1, "V")),
    ("zU", (2, 0, 0, "V")),
    ("zU", (1, 1, 0, "V")),
    ("zSt", (2, 0, "S")),
    ("xQ", (7,)),
    ("ri3", ()),
    ("zU", (3, 1, 1, "V")),
    ("xC", (6, "S")),
    ("xT", (5,)),
    ("xC", (5, "S")),
    ("zM", (1, 0)),
    ("zM", (3, 0)),
    ("zU", (1, 0, 1, "V")),
    ("aT", (0, 0)),
    ("xQ", (6,)),
    ("xQ", (5,)),
    ("zSt", (3, 0, "S")),
    ("zSt", (3, 1, "S")),
    ("zSt", (1, 0, "V")),
    ("zU", (1, 0, 0, "V")),
    ("zT", (1, 2)),
    ("zU", (3, 0, 1, "V")),
    ("zU", (0, 1, 1, "G")),
    ("sS2", (0,)),
    ("zC", (1, 2, "S")),
    ("zM", (2, 1)),
    ("acp", ()),
    ("zT", (1, 3)),
    ("zU", (2, 0, 1, "G")),
    ("zM", (5, 0)),
    ("zU", (2, 1, 1, "V")),
    ("zU", (3, 0, 0, "G")),
    ("zU", (2, 1, 0, "V")),
    ("zU", (3, 1, 0, "G")),
    ("zC", (1, 3, "S")),
    ("sB", (0,)),
    ("zSt", (2, 1, "V")),
    ("zSt", (5, 0, "V")),
    ("zM", (4, 0)),
    ("sS2", (1,)),
    ("acol", ()),
    ("zU", (5, 0, 0, "V")),
    ("sC", (0, "S")),
    ("zT", (1, 0)),
    ("sB", (1,)),
    ("zT", (1, 1)),
    ("zs", (0, 1, 0, "V")),
    ("zSt", (4, 0, "S")),
    ("aT", (0, 1)),
    ("zs", (0, 0, 1, "V")),
    ("zM", (4, 1)),
    ("zs", (0, 0, 0, "G")),
    ("gt", (0, 0)),
    ("zC", (1, 0, "S")),
    ("zM", (7, 0)),
    ("sC", (1, "S")),
    ("cM", (0, 0)),
    ("zC", (1, 1, "S")),
    ("zM", (6, 0)),
    ("zSt", (4, 1, "S")),
    ("zSt", (7, 0, "S")),
    ("zU", (6, 0, 0, "V")),
    ("gt", (0, 1)),
    ("zSt", (6, 0, "S")),
    ("zS", (6,)),
    ("zs", (0, 1, 1, "G")),
    ("zM", (7, 1)),
    ("zU", (4, 0, 0, "G")),
    ("zM", (5, 1)),
    ("zU", (4, 0, 1, "G")),
    ("zSt", (5, 1, "S")),
    ("zU", (7, 0, 0, "V")),
    ("zS", (7,)),
    ("zU", (7, 0, 1, "V")),
    ("zU", (5, 0, 1, "G")),
    ("cM", (0, 1)),
    ("zS", (5,)),
    ("zU", (6, 0, 1, "V")),
    ("zS", (4,)),
    ("cQ", (0, 1)),
    ("zs", (1, 0, 0, "V")),
    ("sS3", (3,)),
    ("sS3", (2,)),
    ("zSt", (7, 1, "S")),
    ("zM", (6, 1)),
    ("aT", (1, 0)),
    ("zs", (1, 0, 1, "V")),
    ("aT", (0, 2)),
    ("zQ", (0, 0)),
    ("zQ", (1, 0)),
    ("zSt", (6, 1, "S")),
    ("sB", (2,)),
    ("gt", (1, 0)),
    ("sC", (2, "S")),
    ("zs", (1, 1, 0, "G")),
    ("cM", (1, 0)),
    ("cQ", (0, 0)),
    ("cQ", (1, 0)),
    ("gt", (0, 2)),
    ("cM", (0, 2)),
    ("aT", (1, 2)),
    ("gt", (1, 2)),
    ("mM", (0, 0, 0)),
    ("aT", (1, 1)),
    ("sB", (3,)),
    ("mM", (0, 0, 1)),
    ("cM", (1, 2)),
    ("zs", (1, 1, 1, "G")),
    ("cQ", (0, 2)),
    ("gt", (1, 1)),
    ("aT", (0, 3)),
    ("sC", (3, "S")),
    ("cQ", (1, 2)),
    ("gt", (1, 3)),
    ("oA", (0, 0, 1, "X")),
    ("cM", (1, 1)),
    ("mM", (1, 0, 1)),
    ("oA", (0, 0, 0, "V")),
    ("aT", (1, 3)),
    ("cQ", (1, 1)),
    ("zQ", (0, 1)),
    ("gt", (0, 3)),
    ("mM", (0, 0, 2)),
    ("oA", (0, 0, 2, "X")),
    ("mM", (0, 0, 3)),
    ("oA", (0, 0, 3, "X")),
    ("zQ", (1, 1)),
    ("cM", (1, 3)),
    ("mM", (1, 0, 0)),
    ("oS", (0, 0, 0)),
    ("oA", (1, 0, 1, "V")),
    ("oA", (1, 0, 0, "V")),
    ("mM", (0, 1, 1)),
    ("cM", (0, 3)),
    ("oA", (0, 1, 1, "V")),
    ("mM", (0, 1, 3)),
    ("mM", (0, 1, 2)),
    ("mM", (0, 1, 0)),
    ("cQ", (0, 3)),
    ("cQ", (1, 3)),
    ("oA", (0, 1, 2, "V")),
    ("mM", (1, 0, 2)),
    ("oA", (0, 1, 3, "X")),
    ("mM", (1, 0, 3)),
    ("oG", (0, 0, 0, "S")),
    ("oA", (0, 1, 0, "V")),
    ("mM", (1, 1, 3)),
    ("oG", (0, 0, 1, "S")),
    ("oA", (1, 0, 2, "V")),
    ("mM", (1, 1, 0)),
    ("oG", (0, 1, 1, "S")),
    ("oA", (1, 0, 3, "V")),
    ("oS", (1, 0, 0)),
    ("oQ", (0, 0)),
    ("oS", (0, 0, 2)),
    ("oG", (0, 1, 0, "S")),
    ("oS", (0, 1, 2)),
    ("oS", (1, 0, 2)),
    ("oP", (0, 0)),
    ("mM", (1, 1, 2)),
    ("mM", (1, 1, 1)),
    ("oP", (0, 1)),
    ("oP", (3, 0)),
    ("oP", (2, 0)),
    ("oP", (1, 1)),
    ("qS", (0, 0)),
    ("oQ", (0, 1)),
    ("oP", (1, 0)),
    ("oGp", (0, 0, "S")),
    ("oG", (1, 0, 0, "S")),
    ("oS", (0, 1, 0)),
    ("oP", (2, 1)),
    ("qS", (0, 1)),
    ("oP", (3, 1)),
    ("oSp", (0,)),
    ("oGp", (1, 1, "V")),
    ("oGp", (0, 1, "V")),
    ("oGp", (1, 0, "V")),
    ("oQp", (0,)),
    ("oG", (1, 0, 1, "G")),
    ("oQp", (1,)),
    ("qSp", (0,)),
    ("oQ", (1, 0)),
    ("qSp", (1,)),
    ("oSp", (1,)),
    ("qS", (1, 0)),
]


def tile_fagcnsignedtanhpropagation_x2_kernel(tc, x, w_words, w_scales, adj, a1, a2, ri, ro, out_0, out_1, out_2):
    nc = tc.nc
    with ExitStack() as ctx:
        keep = ctx.enter_context(tc.tile_pool(name="keep", bufs=1))
        zt_pool = ctx.enter_context(tc.tile_pool(name="zt_pool", bufs=4))
        wide = ctx.enter_context(tc.tile_pool(name="wide", bufs=3))
        wide4 = ctx.enter_context(tc.tile_pool(name="wide4", bufs=4))
        work = ctx.enter_context(tc.tile_pool(name="work", bufs=2))
        ps_tr = ctx.enter_context(tc.psum_pool(name="ps_tr", bufs=2))
        ps_mm = ctx.enter_context(tc.psum_pool(name="ps_mm", bufs=4))
        ps_c = ctx.enter_context(tc.psum_pool(name="ps_c", bufs=1))
        ps_s = ctx.enter_context(tc.psum_pool(name="ps_s", bufs=1))
        ctx.enter_context(tc.manual_schedule())

        x_sb = [keep.tile([128, 4, 1024], BF16, name=f"x_sb{g}", align_bytes=64) for g in range(2)]
        adj_sb = [keep.tile([128, 4, 1024], BF16, name=f"adj_sb{g}", align_bytes=64) for g in range(2)]
        w_codes = keep.tile([128, 2, 2048], U8, name="w_codes", align_bytes=64)
        w_sc = keep.tile([128, 2, 1024], U8, name="w_sc", align_bytes=64)
        a_rows = keep.tile([128, 2, 1024], BF16, name="a_rows", align_bytes=64)
        a_bc = keep.tile([128, 2, 1024], BF16, name="a_bc", align_bytes=64)
        a_col = keep.tile([128, 4, 2], F32, name="a_col", align_bytes=64)
        ones = keep.tile([128, 128], BF16, name="ones", align_bytes=64)
        ident = keep.tile([128, 128], F32, name="ident", align_bytes=64)
        ri_sb = keep.tile([128, 2, 4], BF16, name="ri_sb")
        ro_sb = keep.tile([128, 2, 4], BF16, name="ro_sb")
        ro32 = keep.tile([128, 2, 4], F32, name="ro32")
        ri3 = keep.tile([128, 2, 4], F32, name="ri3")
        dummy = keep.tile([128, 1], F32, name="dummy")
        part = [keep.tile([128, 4, 2, 2], F32, name=f"part{g}") for g in range(2)]
        s_row = keep.tile([128, 1024], F32, name="s_row", align_bytes=64)
        score = [keep.tile([128, 4, 2], F32, name=f"score{g}") for g in range(2)]
        z03 = [keep.tile([128, 4, 1024], F32, name=f"z03_{g}", align_bytes=64) for g in range(2)]
        xq = [keep.tile([128, 2, 512], U32, name=f"xq{g}", align_bytes=64) for g in range(2)]
        xs = [keep.tile([128, 2, 512], U8, name=f"xs{g}", align_bytes=64) for g in range(2)]
        zq = [keep.tile([128, 1024], U32, name=f"zq{g}", align_bytes=64) for g in range(2)]
        zsc = [keep.tile([128, 1024], U8, name=f"zsc{g}", align_bytes=64) for g in range(2)]
        cq = [[keep.tile([128, 512], U32, name=f"cq{j}{i}", align_bytes=64) for i in range(2)] for j in range(2)]
        csc = [[keep.tile([128, 512], U8, name=f"csc{j}{i}", align_bytes=64) for i in range(2)] for j in range(2)]
        o_sb = [keep.tile([128, 4, 1024], F32, name=f"o_sb{g}", align_bytes=64) for g in range(2)]
        oq = [keep.tile([128, 1024], U32, name=f"oq{g}", align_bytes=64) for g in range(2)]
        osc = [keep.tile([128, 1024], U8, name=f"osc{g}", align_bytes=64) for g in range(2)]

        nc.gpsimd.memset(dummy[:], 0.0)
        nc.vector.memset(w_sc[:].bitcast(I32), 0)
        nc.vector.memset(a_rows[:], 0.0)
        nc.vector.memset(ones[:], 1.0)
        make_identity(nc, ident[:])

        def x_view(t_dram, g):
            return t_dram[512 * g : 512 * (g + 1), :].rearrange("(p t) k -> p t k", t=4)

        def load_x(s, n=1):
            g, t = s // 4, s % 4
            nc.sync.dma_start(out=x_sb[g][:, t : t + n, :], in_=x_view(x, g)[:, t : t + n, :])

        load_x(0)
        for r in range(4):
            nc.sync.dma_start(
                out=w_sc[:].bitcast(I32)[r:128:32, :, :],
                in_=w_scales.bitcast(I32).rearrange("g (q r) n -> r q g n", r=4)[r],
            )
        for h in range(2):
            for g in range(2):
                nc.sync.dma_start(
                    out=w_codes[:].bitcast(I32)[:, g, 256 * h : 256 * (h + 1)],
                    in_=w_words.bitcast(I32)[g][:, 256 * h : 256 * (h + 1)],
                )
            if h == 0:
                nc.sync.dma_start(out=a_rows[0:1, 0, :], in_=a1.unsqueeze(0))
                nc.sync.dma_start(out=a_rows[0:1, 1, :], in_=a2.unsqueeze(0))
                load_x(1)
        nc.scalar.activation(out=dummy[:], in_=dummy[:], func=TANH)
        load_x(2, 2)
        load_x(4, 2)
        load_x(6, 2)
        nc.sync.dma_start(out=ri_sb[:], in_=ri.rearrange("(g p t) -> p g t", g=2, t=4))
        nc.sync.dma_start(out=ro_sb[:], in_=ro.rearrange("(g p t) -> p g t", g=2, t=4))
        for g in range(2):
            for h in range(2):
                nc.sync.dma_start(out=adj_sb[g][:, 2 * h : 2 * h + 2, :], in_=x_view(adj, g)[:, 2 * h : 2 * h + 2, :])

        trs = {}
        grp = {}
        zps = {}
        zts = {}

        def x_transpose(s):
            g, t = s // 4, s % 4
            words = x_sb[g][:, t, :].bitcast(F32)
            tr = ps_tr.tile([128, 2, 2, 128], F32, name="tr")
            for k in range(2):
                for u in range(2):
                    nc.tensor.transpose(tr[:, k, u, :], words[:, 256 * k + u : 256 * (k + 1) : 2], ident[:])
            trs[s] = tr

        def x_copy(s, eng="S"):
            xg = wide.tile([128, 2, 128, 4], BF16, name="xg", align_bytes=64)
            dst = xg[:].rearrange("p k r t -> p (k r t)").bitcast(F32).rearrange("p (k r u) -> p k r u", k=2, u=2)
            src = trs[s][:].rearrange("p k u r -> p k r u")
            if eng == "S":
                nc.scalar.copy(out=dst, in_=src)
            else:
                nc.vector.tensor_copy(out=dst, in_=src)
            grp[s] = xg

        def x_quant(s):
            for k in range(2):
                nc.vector.quantize_mx(
                    out=xq[s // 4][:, k, 128 * (s % 4) : 128 * (s % 4 + 1)].bitcast(FP8X4),
                    scales=xs[s // 4][:, k, 128 * (s % 4) : 128 * (s % 4 + 1)],
                    in_=grp[s][:, k, :, :].rearrange("p r t -> p (r t)"),
                )

        def z_mm(s, h):
            zp = ps_mm.tile([128, 512], F32, name="mm")
            for k in range(2):
                nc.tensor.matmul_mx(
                    out=zp[:],
                    lhsT=xq[s // 4][:, k, 128 * (s % 4) : 128 * (s % 4 + 1)].bitcast(FP8X4),
                    lhsT_scale=xs[s // 4][:, k, 128 * (s % 4) : 128 * (s % 4 + 1)],
                    rhs=w_codes[:, k, 1024 * h : 1024 * (h + 1)].bitcast(FP4X4),
                    rhs_scale=w_sc[:, k, 512 * h : 512 * (h + 1)],
                    start=(k == 0),
                    stop=(k == 1),
                )
            zps[s, h] = zp

        sc = ps_c.tile([128, 4, 2], F32, name="sc")
        zts = {}

        def zt_mm(g, n):
            zp = ps_mm.tile([128, 512], F32, name="mm")
            for k in range(2):
                nc.tensor.matmul_mx(
                    out=zp[:],
                    lhsT=w_codes[:, k, 1024 + 256 * n : 1024 + 256 * (n + 1)].bitcast(FP4X4),
                    lhsT_scale=w_sc[:, k, 512 + 128 * n : 512 + 128 * (n + 1)],
                    rhs=xq[g][:, k, :].bitcast(FP8X4),
                    rhs_scale=xs[g][:, k, :],
                    start=(k == 0),
                    stop=(k == 1),
                )
            zps[g, n, "t"] = zp

        def zt_copy(g, n, eng="S"):
            zt = zt_pool.tile([128, 512], F32, name="zt", align_bytes=64)
            if eng == "S":
                nc.scalar.copy(out=zt[:], in_=zps[g, n, "t"][:])
            else:
                nc.vector.tensor_copy(out=zt[:], in_=zps[g, n, "t"][:])
            zts[g, n] = zt

        def zt_score(s):
            g, t = s // 4, s % 4
            for n in range(4):
                nc.tensor.matmul(
                    sc[:, t, :], lhsT=zts[g, n][:, 128 * t : 128 * (t + 1)], rhs=a_col[:, n, :], start=(n == 0), stop=(n == 3)
                )

        def z_store(s, h, eng="S"):
            g, t = s // 4, s % 4
            dst = z03[g][:, t, 512 * h : 512 * (h + 1)]
            if eng == "S":
                nc.scalar.activation(out=dst, in_=zps[s, h][:], func=COPY, scale=EPS)
            else:
                nc.vector.tensor_scalar(out=dst, in0=zps[s, h][:], scalar1=EPS, scalar2=None, op0=MULT)

        def unit_cols(h):
            return slice(512 * h, 512 * (h + 1))

        def score_unit(s, h, q, eng="V"):
            g, t = s // 4, s % 4
            acc = part[g][:, t, q, h : h + 1]
            if eng == "V":
                junk = work.tile([128, 512], F32, name="junk")
                nc.vector.scalar_tensor_tensor(
                    out=junk[:],
                    in0=zps[s, h][:],
                    scalar=1.0,
                    in1=a_bc[:, q, unit_cols(h)],
                    op0=MULT,
                    op1=MULT,
                    accum_out=acc,
                )
            else:
                pr = wide.tile([128, 512], F32, name="pr")
                nc.gpsimd.tensor_tensor(out=pr[:], in0=z03[g][:, t, unit_cols(h)], in1=a_bc[:, q, unit_cols(h)], op=MULT)
                jk = work.tile([128, 512], F32, name="jk")
                nc.scalar.activation(out=jk[:], in_=pr[:], func=COPY, scale=1.0 / EPS, accum_out=acc)

        def score_sum_units(n):
            g, ts = n // 2, slice(2 * (n % 2), 2 * (n % 2) + 2)
            nc.vector.tensor_reduce(out=score[g][:, ts, :], in_=part[g][:, ts, :, :], axis=mybir.AxisListType.X, op=ADD)

        def score_sum_psum(n):
            g, ts = n // 2, slice(2 * (n % 2), 2 * (n % 2) + 2)
            nc.vector.tensor_tensor(out=score[g][:, ts, :], in0=sc[:, ts, :], in1=part[g][:, ts, :, 0], op=ADD)

        gates = {}
        sps = {}

        def s_bcast(n):
            bank = ps_s.tile([128, 256], F32, name="sp")
            for b in range(2):
                nc.tensor.transpose(
                    bank[:, 128 * b : 128 * (b + 1)],
                    score[n // 2][:, 2 * (n % 2) + b, 0:1].to_broadcast([128, 128]),
                    ident[:],
                )
            sps[n] = bank

        def s_copy(n, eng="S"):
            dst = s_row[:, 256 * n : 256 * (n + 1)]
            if eng == "S":
                nc.scalar.copy(out=dst, in_=sps[n][:])
            else:
                nc.vector.tensor_copy(out=dst, in_=sps[n][:])

        def gate(j, n):
            gt = wide.tile([128, 4, 256], F32, name="gate", align_bytes=64)
            for t in range(4):
                nc.scalar.activation(
                    out=gt[:, t, :], in_=s_row[:, 256 * n : 256 * (n + 1)], func=TANH, bias=score[j][:, t, 1:2]
                )
            gates[j, n] = gt

        zgt = {}

        def zs_piece(g, h, c, eng="V"):
            if (g, h) not in zgt:
                zgt[g, h] = wide4.tile([128, 512, 4], BF16, name="zg", align_bytes=64)
            parts, on = (1, nc.vector) if eng == "V" else (2, nc.gpsimd)
            wid = 256 // parts
            for n in range(parts):
                lo = 256 * c + wid * n
                on.tensor_tensor(
                    out=zgt[g, h][:, lo : lo + wid, :],
                    in0=z03[g][:, :, 512 * h + lo : 512 * h + lo + wid].rearrange("p t f -> p f t"),
                    in1=ri3[:, g, :].unsqueeze(1).to_broadcast([128, wid, 4]),
                    op=MULT,
                )

        def zs_quant(g, h):
            nc.vector.quantize_mx(
                out=zq[g][:, 512 * h : 512 * (h + 1)].bitcast(FP8X4),
                scales=zsc[g][:, 512 * h : 512 * (h + 1)],
                in_=zgt[g, h][:].rearrange("p f t -> p (f t)"),
            )

        def adj_transpose(j, n):
            tr = ps_tr.tile([128, 2, 256], F32, name="tr")
            for b in range(2):
                words = adj_sb[n // 2][:, 2 * (n % 2) + b, :].bitcast(F32)
                for u in range(2):
                    nc.tensor.transpose(tr[:, u, 128 * b : 128 * (b + 1)], words[:, 256 * j + u : 256 * (j + 1) : 2], ident[:])
            trs[j, n] = tr

        cgs = {}

        def c_mul(j, n):
            cg = wide.tile([128, 256, 4], BF16, name="cg", align_bytes=64)
            nc.vector.tensor_tensor(
                out=cg[:].rearrange("p n (u e) -> p n u e", u=2),
                in0=trs[j, n][:].rearrange("p u n -> p (u n)").bitcast(BF16).rearrange("p (u n e) -> p n u e", u=2, e=2),
                in1=gates[j, n][:].rearrange("p (u e) n -> p n u e", u=2),
                op=MULT,
            )
            cgs[j, n] = cg

        def c_quant(j, n):
            cols = slice(256 * (n % 2), 256 * (n % 2) + 256)
            nc.vector.quantize_mx(
                out=cq[j][n // 2][:, cols].bitcast(FP8X4),
                scales=csc[j][n // 2][:, cols],
                in_=cgs[j, n][:].rearrange("p n t -> p (n t)"),
            )

        mps = {}

        def m_mm(g, h, t):
            mp = ps_mm.tile([128, 512], F32, name="mm")
            for j in range(2):
                nc.tensor.matmul_mx(
                    out=mp[:],
                    lhsT=cq[j][g][:, 128 * t : 128 * (t + 1)].bitcast(FP8X4),
                    lhsT_scale=csc[j][g][:, 128 * t : 128 * (t + 1)],
                    rhs=zq[j][:, 512 * h : 512 * (h + 1)].bitcast(FP8X4),
                    rhs_scale=zsc[j][:, 512 * h : 512 * (h + 1)],
                    start=(j == 0),
                    stop=(j == 1),
                )
            mps[g, h, t] = mp

        def o_add(g, h, t, eng="V"):
            cols = slice(512 * h, 512 * (h + 1))
            if eng == "V":
                nc.vector.scalar_tensor_tensor(
                    out=o_sb[g][:, t, cols],
                    in0=mps[g, h, t][:],
                    scalar=ro_sb[:, g, t : t + 1],
                    in1=z03[g][:, t, cols],
                    op0=MULT,
                    op1=ADD,
                )
            else:
                mr = wide.tile([128, 512], F32, name="mr", align_bytes=64)
                nc.scalar.activation(out=mr[:], in_=mps[g, h, t][:], func=COPY, scale=ro32[:, g, t : t + 1])
                nc.gpsimd.tensor_tensor(out=o_sb[g][:, t, cols], in0=mr[:], in1=z03[g][:, t, cols], op=ADD)

        def o_add_part(t, c):
            cols = slice(512 + 256 * c, 512 + 256 * (c + 1))
            nc.vector.scalar_tensor_tensor(
                out=o_sb[1][:, t, cols],
                in0=mps[1, 1, t][:, 256 * c : 256 * (c + 1)],
                scalar=ro_sb[:, 1, t : t + 1],
                in1=z03[1][:, t, cols],
                op0=MULT,
                op1=ADD,
            )

        ogs = {}

        def o_group_cols(g, h, lo, wid, eng):
            if (g, h) not in ogs:
                ogs[g, h] = wide.tile([128, 512, 4], BF16, name="og", align_bytes=64)
            src = o_sb[g][:, :, 512 * h + lo : 512 * h + lo + wid].rearrange("p t f -> p f t")
            dst = ogs[g, h][:, lo : lo + wid, :]
            if eng == "S":
                nc.scalar.copy(out=dst, in_=src)
            elif eng == "V":
                nc.vector.tensor_copy(out=dst, in_=src)
            else:
                nc.gpsimd.tensor_scalar(out=dst, in0=src, scalar1=1.0, scalar2=0.0, op0=MULT, op1=ADD)

        def o_group(g, h, c, eng="S"):
            o_group_cols(g, h, 256 * c, 256, eng)

        def o_group_part(c, n, eng="S"):
            o_group_cols(1, 1, 256 * c + 128 * n, 128, eng)

        def o_quant_cols(g, h, lo, wid):
            cols = slice(512 * h + lo, 512 * h + lo + wid)
            nc.vector.quantize_mx(
                out=oq[g][:, cols].bitcast(FP8X4),
                scales=osc[g][:, cols],
                in_=ogs[g, h][:, lo : lo + wid, :].rearrange("p n t -> p (n t)"),
            )

        def o_quant(g, h):
            o_quant_cols(g, h, 0, 512)

        def o_quant_part(c):
            o_quant_cols(1, 1, 256 * c, 256)

        def o_store(g, h, t):
            cols = slice(512 * h, 512 * (h + 1))
            nc.sync.dma_start(out=x_view(out_0, g)[:, t : t + 2, cols], in_=o_sb[g][:, t : t + 2, cols])

        def o_store_part(c):
            cols = slice(512 + 256 * c, 512 + 256 * (c + 1))
            nc.sync.dma_start(out=x_view(out_0, 1)[:, :, cols], in_=o_sb[1][:, :, cols])

        def code_store(g, lo, hi):
            nc.sync.dma_start(
                out=out_1[g].rearrange("p m t -> p (m t)").bitcast(I32)[:, lo:hi],
                in_=oq[g][:, lo:hi].bitcast(I32),
            )

        def scale_store(g, lo, hi):
            for r in range(4):
                nc.sync.dma_start(
                    out=out_2[g].bitcast(I32).rearrange("(q r) n -> r q n", r=4)[r][:, lo // 4 : hi // 4],
                    in_=osc[g][:].bitcast(I32)[r:128:32, lo // 4 : hi // 4],
                )

        def q_store(g, h):
            code_store(g, 512 * h, 512 * (h + 1))
            scale_store(g, 512 * h, 512 * (h + 1))

        def q_store_part(c):
            code_store(1, 512 + 256 * c, 512 + 256 * (c + 1))
            if c == 1:
                scale_store(1, 512, 1024)

        def a_rows_to_all():
            for q in range(2):
                for h in range(2):
                    ap = ps_mm.tile([128, 512], F32, name="mm")
                    nc.tensor.matmul(ap[:], lhsT=ones[:], rhs=a_rows[:, q, 512 * h : 512 * (h + 1)], start=True, stop=True)
                    dst = a_bc[:, q, 512 * h : 512 * (h + 1)]
                    if h == 0:
                        nc.vector.tensor_copy(out=dst, in_=ap[:])
                    else:
                        nc.scalar.copy(out=dst, in_=ap[:])

        acps = {}

        def a_to_columns():
            acp = ps_mm.tile([128, 4, 2], F32, name="mm")
            for n in range(4):
                for q in range(2):
                    nc.tensor.matmul(
                        acp[:, n, q : q + 1],
                        lhsT=a_rows[:, q, 512 + 128 * n : 512 + 128 * (n + 1)],
                        rhs=ones[:, 0:1],
                        start=True,
                        stop=True,
                    )
            acps[0] = acp

        def a_columns_copy():
            nc.vector.tensor_copy(out=a_col[:], in_=acps[0][:])

        def node_scales():
            nc.gpsimd.tensor_scalar(out=ri3[:], in0=ri_sb[:], scalar1=1.0 / EPS, scalar2=None, op0=MULT)
            nc.gpsimd.tensor_copy(out=ro32[:], in_=ro_sb[:])

        steps = {
            "abc2": a_rows_to_all, "acp": a_to_columns, "acol": a_columns_copy, "ri3": node_scales,
            "xT": x_transpose, "xC": x_copy, "xQ": x_quant, "zM": z_mm, "zU": score_unit, "zSt": z_store,
            "zT": zt_mm, "zC": zt_copy, "zS": zt_score, "sS2": score_sum_units, "sS3": score_sum_psum,
            "sB": s_bcast, "sC": s_copy, "gt": gate, "aT": adj_transpose, "cM": c_mul, "cQ": c_quant,
            "zs": zs_piece, "zQ": zs_quant, "mM": m_mm, "oA": o_add, "oP": o_add_part, "oG": o_group,
            "oGp": o_group_part, "oQ": o_quant, "oQp": o_quant_part, "oS": o_store, "oSp": o_store_part,
            "qS": q_store, "qSp": q_store_part,
        }
        for name, args in ORDER:
            steps[name](*args)
